import numpy as np, ml_dtypes
CORES = [10,34,74,98]
N = 4
import mx_ref
BF = ml_dtypes.bfloat16
def entries(a):
    return np.ascontiguousarray(a.T).reshape(-1)
def table(e):
    return np.ascontiguousarray(np.reshape(e, (-1, 16)).T).astype(np.int32)
def f(rng, *shape):
    return mx_ref.flush((rng.standard_normal(shape, dtype=np.float32) * np.exp2(rng.integers(-2, 3, shape[:-1] + (1,)))).astype(BF))
def wide(rng, *shape, cols=0):
    v = rng.standard_normal(shape, dtype=np.float32) * np.exp2(rng.integers(-12, 13, shape)).astype(np.float32)
    if cols: v *= np.repeat(np.exp2(rng.integers(-cols, cols + 1, shape[:-2] + (1, shape[-1] // 4))) * (rng.random(shape[:-2] + (1, shape[-1] // 4)) > 0.0625), 4, axis=-1).astype(np.float32)
    return mx_ref.flush(v.astype(BF))
T, ND, CD, LM, CAPP = 1024, 64, 16, 64, 144
def lens(rng, n, total):
    a = 1 + np.minimum(LM - 1, rng.multinomial(total - n, rng.dirichlet(np.ones(n))))
    for i in rng.permutation(n): a[i] += min(LM - a[i], total - a.sum())
    return a
def places(rng, l):
    o = rng.permutation(ND); g = rng.multinomial(T - l.sum(), rng.dirichlet(np.ones(ND + 1)))
    s = np.zeros(ND, int); s[o] = np.cumsum(g[:ND]) + np.cumsum(l[o]) - l[o]
    return s
def pick(rng, l):
    p = rng.permutation(ND); a, b = p[:CD].copy(), p[CD:].copy()
    while l[a].sum() > CAPP:
        i = np.argmax(l[a]); j = rng.choice(np.flatnonzero(l[b] < l[a[i]]))
        a[i], b[j] = b[j], a[i]
    return rng.permutation(a)
def lists(rng, kind="any"):
    s, n, c = [], [], np.zeros((N, N * CD), int)
    K, J = (T - ND) // (LM - 1), (CAPP - CD) // (LM - 1)
    TT = min(T, ND // CD * CAPP)
    for q in range(N):
        d = rng.permutation(ND); l = np.ones(ND, int)
        if kind == "long": l[d[:K]] = LM
        elif kind == "full": l[d] = np.concatenate([lens(rng, CD, CAPP), lens(rng, CD, CAPP), lens(rng, ND - 2 * CD, T - 2 * CAPP)])
        elif kind == "any": l[d] = lens(rng, ND, int(rng.integers(TT - TT // 4, TT + 1)))
        s.append(table(places(rng, l))); n.append(table(l))
        for r in range(N):
            if kind == "long": e = rng.permutation(np.concatenate([rng.permutation(d[:K])[:J], rng.permutation(d[K:])[:CD - J]]))
            elif kind == "full": k = CD * int(rng.integers(0, 2)); e = rng.permutation(d[k:k + CD])
            else: e = pick(rng, l)
            c[r, CD * q:CD * q + CD] = e
    return {"st": np.stack(s), "ln": np.stack(n), "cd": np.stack([table(c[r]) for r in range(N)])}
def setup_inputs(rng):
    return {"x": f(rng, N, 128, 4 * T), "qw": f(rng, N, 128, 512), **lists(rng)}
def setup_inputs_long(rng):
    return {**setup_inputs(rng), **lists(rng, "long")}
def setup_inputs_ones(rng):
    return {**setup_inputs(rng), **lists(rng, "ones")}
def setup_inputs_full(rng):
    return {**setup_inputs(rng), **lists(rng, "full")}
def setup_inputs_below(rng):
    d = setup_inputs(rng); p = rng.permutation(N)
    s, u = rng.integers(-20, 27, N), rng.integers(-20, 28, N)
    s[p[0]] = 26; u[rng.choice(p[:-1])] = 27; s[p[-1]] = 0; u[p[-1]] = 0
    d["x"] = mx_ref.flush((-np.exp2(rng.uniform(-3, 3, (N, 128, 4 * T)) + s[:, None, None])).astype(BF))
    d["qw"] = mx_ref.flush(np.exp2(rng.uniform(-2, 2, (N, 128, 512)) + u[:, None, None]).astype(BF))
    return d
def setup_inputs_spread(rng):
    d = setup_inputs(rng); d["x"] = wide(rng, N, 128, 4 * T, cols=8); return d
def check_inputs(d):
    b = []
    L = [entries(d["ln"][r]).astype(np.int64) for r in range(N)]
    for r in range(N):
        s, l = entries(d["st"][r]).astype(np.int64), L[r]
        if l.min() < 1 or l.max() > LM: b.append("ln")
        o = np.argsort(s, kind="stable")
        if s.min() < 0 or (s + l).max() > T or (s[o][:-1] + l[o][:-1] > s[o][1:]).any(): b.append("st")
        c = entries(d["cd"][r])
        if c.min() < 0 or c.max() >= ND: b.append("cd"); continue
        for q in range(N):
            e = c[CD * q:CD * q + CD]
            if len(set(e.tolist())) != CD or L[q][e].sum() > CAPP: b.append("cd")
    return sorted(set(b))
def reference(x, qw, st, ln, cd):
    X = [mx_ref.quantize(x[q]) for q in range(N)]
    y = np.zeros((N, 128, N * CD), np.float32)
    for r in range(N):
        W = mx_ref.quantize(qw[r]); c = entries(cd[r])
        for q in range(N):
            z = mx_ref.matmul(W, X[q]); s, l = entries(st[q]), entries(ln[q])
            for i in range(CD * q, CD * q + CD):
                y[r][:, i] = z[:, s[c[i]]:s[c[i]] + l[c[i]]].max(axis=1)
    return {"y": y}

@@ -1,0 +1,263 @@
+import numpy as np
+from concourse.bass import DstId, RemoteDMATransfer
+from concourse.mybir import dt, AluOpType, ActivationFunctionType
+
+CAP = 144
+WIN = 152
+KO = CAP // 4
+ND, CD, XC = 64, 16, 1024
+XA = 1408
+CUT = 16
+LOW = -1.0e29
+HOLD = 8192
+
+F, I, U, B = "float32", "int32", "uint16", "bfloat16"
+SCRATCH = {n: ("sbuf", [128, w], d) for n, w, d in [
+    ("xw", 4 * (XC + CAP), B), ("qt", 512, B), ("tile", 16 * CAP, B),
+    ("qwc", 128, "float8_e4m3fn_x4"), ("qws", 128, "uint8"), ("qc", 4 * CAP, "float8_e4m3fn_x4"), ("qs", 4 * CAP, "uint8"),
+    ("lc", 3 * CAP, "float8_e4m3fn_x4"), ("lp", 3 * CAP, "uint8"),
+    ("cdl", 4, I), ("cds", 4, U), ("lst", 12, U), ("lo", 4, U),
+    ("row", 128, I), ("bc", 128, I), ("stw", 64, F), ("lnw", 64, F), ("nl", 64, F), ("nen", 64, F),
+    ("MG", 64, F), ("C", 64, F), ("ST", 72, F), ("J", 64, F), ("cL", 8, U), ("seL", 6, U),
+    ("D", 4 * WIN, F), ("SS", 4 * CAP, F), ("XX", 4 * CAP, F), ("O", CAP, U),
+    ("mask", 4 * WIN, F), ("Z", 4 * WIN, F), ("yo", 64, F), ("neg", 16, F),
+    ("lrow", 96, F), ("lcol", 96, F), ("u16", 64, F), ("u4", CAP, F), ("pc", 8, F), ("po", 8, U),
+    ("tri", 64, F), ("resm", 64, F), ("A", CAP, F), ("four", CAP, F)]}
+SCRATCH["ps"] = ("psum", [128, 2048], F)
+SEMAPHORES = ["ldcd", "ldtab", "ldqw", "ldxa", "ldxb", "v", "s", "pe", "gi", "go", "lst", "sel",
+              "arr0", "arr1", "arr2", "snt", "yst"]
+
+ADD, SUB, MUL, MAX, MIN = AluOpType.add, AluOpType.subtract, AluOpType.mult, AluOpType.max, AluOpType.min
+
+
+def bits(engines):
+    return sum(1 << e for e in engines)
+
+
+def rank_program(g, core, T, topo):
+    rank = T.rank_of(core)
+    if rank is None:
+        return
+    V, S, P, Y = g.vector, g.scalar, g.tensor, g.sync
+    Copy = ActivationFunctionType.Copy
+    chips = [topo.chip(c) for c in T.cores]
+    steps = sorted([1, 3, 2], key=lambda v: 1 if topo.same_plane(chips[0], chips[v]) else 0)
+    part = [rank ^ v for v in steps]
+    addr = [topo.addr(T.cores[p]) for p in part]
+    eng = [topo.engines(core, T.cores[p]) for p in part]
+    dsts = [DstId(rid=a[0], pnc=a[1]) for a in addr]
+    both = [e for e in eng[0] if e in eng[1] and e in eng[2]]
+    ne, h = len(both), len(both) // 2
+
+    cnt, seen = {}, {}
+
+    def done(ins, name, n=1):
+        ins.then_inc(T.sem[name], n)
+        cnt[name] = cnt.get(name, 0) + n
+        return (name, cnt[name])
+
+    def need(qn, q, *toks):
+        for name, val in toks:
+            if seen.get((qn, name), 0) < val:
+                q.wait_ge(T.sem[name], val)
+                seen[(qn, name)] = val
+
+    def vneed(*toks):
+        need("v", V, *toks)
+
+    def v(ins):
+        return done(ins, "v")
+
+    for k in range(8):
+        q = Y if k < 4 else S
+        done(q.dma_start(T.cdl[16 * k:16 * k + 16, :], T.cd[:]), "ldcd", 16)
+    done(S.dma_start(T.row[0:1, 0:64], T.st[:]), "ldtab", 16)
+    done(S.dma_start(T.row[0:1, 64:128], T.ln[:]), "ldtab", 16)
+    t_cd, t_tab = ("ldcd", 128), ("ldtab", 32)
+    t_xa = done(Y.dma_start(T.xw[:, 0:XA], T.x[:, 0:XA]), "ldxa", 16)
+    Y.wait_ge(T.sem.go, 1)
+    t_xb = done(Y.dma_start(T.xw[:, XA:4 * XC], T.x[:, XA:4 * XC]), "ldxb", 16)
+    t_qw = done(Y.dma_start(T.qt[:], T.qw[:]), "ldqw", 16)
+
+    def iota(out, pattern, base=0):
+        return done(g.iota(out, pattern, base, 0, allow_small_or_imprecise_dtypes=True), "gi")
+
+    iota(T.lrow[:, 0:32], [[0, 2], [4, 16]])
+    iota(T.lrow[:, 32:64], [[0, 2], [2 * HOLD, 4], [0, 4]])
+    i_row = iota(T.lrow[:, 64:96], [[0, 2], [-HOLD, 4], [-1, 4]], 3 * HOLD)
+    i_u16 = iota(T.u16[:], [[0, 4], [4, 16]])
+    i_pc = iota(T.pc[:], [[64, 2], [1, 4]])
+    i_u4 = iota(T.u4[:], [[0, KO], [2 * HOLD, 4]], -HOLD)
+    lane4, turn, sub = T.lcol[:, 0:1], T.lcol[:, 32:33], T.lcol[:, 64:65]
+
+    v(V.memset(T.D[:], 0.0))
+    v(V.memset(T.xw[:, 4 * XC:4 * (XC + CAP)], 0.0))
+    v(V.memset(T.ST[:, 64:72], 0.0))
+    vneed(i_row)
+    t = v(V.transpose(T.lcol[:], T.lrow[:]))
+    v(V.memset(T.four[:], 4.0))
+    vneed(t, i_u16)
+    v(V.tensor_scalar(T.tri[:], T.u16[:], lane4, None, AluOpType.is_le))
+    v(V.tensor_scalar(T.resm[:], T.u16[:], 0.0, None, AluOpType.is_gt))
+    vneed(i_pc)
+    t_po = v(V.tensor_scalar(T.po[:], T.pc[:], lane4, None, ADD))
+    vneed(i_u4)
+    t_a = v(V.tensor_scalar(T.A[:], T.u4[:], turn, float(HOLD), SUB, MIN))
+
+    vneed(t_cd)
+    t = v(V.tensor_copy(T.cds[:], T.cdl[:]))
+    need("g", g, t)
+    g.remote_dma_fused([RemoteDMATransfer(dst_ids=dsts, dma_engine_mask=bits(both), remote_sem=T.sem.lst, srcs=[T.cds[:]],
+                                          dsts=[T.lst[:, 4 * s:4 * s + 4] for s in range(3)])], local_sem=T.sem.snt)
+    nsent = ne
+    g.sem_inc(T.sem.go, 1)
+    need("g", g, t_tab)
+    i_bc = done(g.partition_broadcast(T.bc[:], T.row[0:1, :], 128), "gi")
+
+    v(V.tensor_copy(T.lo[:, 3:4], T.cdl[:, rank:rank + 1]))
+    vneed(t_a)
+    t_const = v(V.memset(T.A[:, 0:CAP:4], -8.0 * HOLD))
+    v(V.memset(T.mask[:], 0.0))
+    v(V.memset(T.neg[:], LOW))
+    t_z = v(V.memset(T.Z[:, 0:4 * WIN:WIN], 0.0))
+
+    vneed(i_bc, t_po)
+    t_ln = v(V.tensor_copy(T.lnw[:], T.bc[:].indirect(T.po[:, 4:8])))
+    t_stw = v(V.tensor_scalar(T.stw[:], T.bc[:].indirect(T.po[:, 0:4]), 4.0, -4.0, MUL, ADD))
+    vneed(t_ln)
+    t = v(V.tensor_scalar(T.nl[:], T.lnw[:], -4.0, None, MUL))
+    vneed(t_stw, t)
+    t_nen = v(V.tensor_tensor(T.nen[:], T.nl[:], T.stw[:], SUB))
+
+    vneed(("lst", 3 * ne))
+    t_lo = v(V.tensor_copy(T.lo[:, 0:3], T.lst[:, rank:12:4]))
+    need("s", S, t_lo)
+    t_st = done(S.activation(T.ST[:, 0:64], T.stw[:].indirect(T.lo[:]), Copy), "s")
+    vneed(t_lo)
+    t = v(V.tensor_tensor(T.MG[:], T.lnw[:].indirect(T.lo[:]), T.tri[:], MUL))
+    vneed(t)
+    t = v(V.tensor_tensor_scan(T.C[:], T.resm[:], T.MG[:], 0.0, MUL, ADD))
+    vneed(t_st, t_nen)
+    v(V.tensor_tensor(T.J[:], T.nen[:].indirect(T.lo[:]), T.ST[:, 1:65], ADD))
+    vneed(t)
+    t_c = v(V.tensor_copy(T.cL[:, 0:8:2], T.C[:, 15:64:16]))
+
+    need("g", g, t_c)
+    share = [both[:h], both[h:h + h // 2], both[h + h // 2:]]
+    g.remote_dma_fused([RemoteDMATransfer(dst_ids=[dsts[s]], dma_engine_mask=bits(share[s]), remote_sem=T.sem.sel,
+                                          srcs=[T.cL[:, 2 * s:2 * s + 1]], dsts=[T.seL[:, 2 * s:2 * s + 1]])
+                        for s in range(3)], local_sem=T.sem.snt)
+    nsent += ne
+
+    def jumps(k):
+        vneed(t_c)
+        return v(V.tensor_copy(T.D[:, WIN * k:WIN * k + CAP + 1].indirect(T.cL[:, 2 * k:2 * k + 1]), T.J[:, 16 * k:16 * k + 16]))
+
+    def run(k, t):
+        vneed(t)
+        return v(V.tensor_tensor_scan(T.SS[:, CAP * k:CAP * k + CAP], T.four[:], T.D[:, WIN * k:WIN * k + CAP],
+                                      T.ST[:, 16 * k:16 * k + 1], ADD, ADD))
+
+    def hold(k, t):
+        vneed(t)
+        return v(V.tensor_tensor_scan(T.XX[:, CAP * k:CAP * k + CAP], T.A[:], T.SS[:, CAP * k:CAP * k + CAP], 0.0, ADD, MAX))
+
+    def offsets(k, t):
+        vneed(t)
+        return v(V.tensor_scalar(T.O[:, KO * k:KO * k + KO], T.XX[:, CAP * k + 3:CAP * k + CAP:4], sub, None, SUB))
+
+    def piece(k, a, b):
+        return (T.tile[:, 4 * CAP * k + 16 * a:4 * CAP * k + 16 * b], T.xw[:].indirect(T.O[:, KO * k + a:KO * k + b]))
+
+    def gather_s(k, t_o):
+        need("s", S, t_o, t_xa, t_xb)
+        o, i = piece(k, CUT, KO)
+        return done(S.activation(o, i, Copy), "s")
+
+    def gather_v(k, t_o):
+        vneed(t_o, t_xa, t_xb)
+        o, i = piece(k, 0, CUT)
+        return v(V.tensor_copy(o, i))
+
+    def quant(k, *toks):
+        vneed(*toks)
+        return v(V.quantize_mx(T.qc[:, CAP * k:CAP * k + CAP], T.qs[:, CAP * k:CAP * k + CAP],
+                               T.tile[:, 4 * CAP * k:4 * CAP * (k + 1)]))
+
+    def send_codes(s, t):
+        need("g", g, t)
+        lo, hi = CAP * s, CAP * s + CAP
+        g.remote_dma(T.lc[:, lo:hi].bitcast(dt.uint8), T.qc[:, lo:hi].bitcast(dt.uint8), T.sem["arr%d" % s], T.sem.snt,
+                     addr[s][1], addr[s][0], bits(both))
+        return ne
+
+    a0 = jumps(0)
+    a1 = jumps(1)
+    b0 = run(0, a0)
+    a2 = jumps(2)
+    c0 = hold(0, b0)
+    b1 = run(1, a1)
+    o0 = offsets(0, c0)
+    c1 = hold(1, b1)
+    b2 = run(2, a2)
+    o1 = offsets(1, c1)
+    c2 = hold(2, b2)
+    s0 = gather_s(0, o0)
+    s1 = gather_s(1, o1)
+    o2 = offsets(2, c2)
+    s2 = gather_s(2, o2)
+    v0 = gather_v(0, o0)
+    nsent += send_codes(0, quant(0, v0, s0))
+    v1 = gather_v(1, o1)
+    nsent += send_codes(1, quant(1, v1, s1))
+    g.remote_dma_fused([RemoteDMATransfer(dst_ids=[dsts[s]], dma_engine_mask=bits(both[h * s:h * s + h]),
+                                          remote_sem=T.sem["arr%d" % s], srcs=[T.qs[:, CAP * s:CAP * s + CAP]],
+                                          dsts=[T.lp[:, CAP * s:CAP * s + CAP]]) for s in range(2)], local_sem=T.sem.snt)
+    nsent += ne
+    v2 = gather_v(2, o2)
+    nsent += send_codes(2, quant(2, v2, s2))
+    g.remote_dma(T.lp[:, 2 * CAP:3 * CAP], T.qs[:, 2 * CAP:3 * CAP], T.sem.arr2, T.sem.snt, addr[2][1], addr[2][0], bits(both))
+    nsent += ne
+    n_arr = [ne + h, ne + h, 2 * ne]
+
+    def ends(k):
+        return T.cL[:, 6:7] if k == 3 else T.seL[:, 2 * k:2 * k + 1]
+
+    def marks(k):
+        vneed(t_z)
+        return v(V.tensor_copy(T.mask[:, WIN * k:WIN * k + CAP + 1].indirect(ends(k)), T.neg[:]))
+
+    t_mk = {}
+    a3 = jumps(3)
+    t_mk[3] = marks(3)
+    b3 = run(3, a3)
+    vneed(t_qw)
+    t_q = v(V.quantize_mx(T.qwc[:], T.qws[:], T.qt[:]))
+    c3 = hold(3, b3)
+    vneed(("sel", ne))
+    t_mk[0] = marks(0)
+    o3 = offsets(3, c3)
+    t_mk[1] = marks(1)
+    s3 = gather_s(3, o3)
+    v3 = gather_v(3, o3)
+    t_mk[2] = marks(2)
+    t_q3 = quant(3, v3, s3)
+
+    need("p", P, t_q)
+    for k in (3, 0, 1, 2):
+        if k == 3:
+            need("p", P, t_q3)
+            rc, rp, q = T.qc[:, 3 * CAP:4 * CAP], T.qs[:, 3 * CAP:4 * CAP], rank
+        else:
+            need("p", P, ("arr%d" % k, n_arr[k]))
+            rc, rp, q = T.lc[:, CAP * k:CAP * k + CAP], T.lp[:, CAP * k:CAP * k + CAP], part[k]
+        t = done(P.matmul_mx(T.ps[:, 512 * k:512 * k + CAP], T.qwc[:], T.qws[:], rc, rp, True, True), "pe")
+        vneed(t, t_mk[k])
+        t = v(V.tensor_tensor_scan(T.Z[:, WIN * k + 1:WIN * k + 1 + CAP], T.mask[:, WIN * k:WIN * k + CAP],
+                                   T.ps[:, 512 * k:512 * k + CAP], LOW, ADD, MAX))
+        vneed(t)
+        t = v(V.tensor_copy(T.yo[:, CD * q:CD * q + CD], T.Z[:, WIN * k:WIN * k + CAP + 1].indirect(ends(k))))
+        need("y", Y, t)
+        done(Y.dma_start(T.y[:, CD * q:CD * q + CD], T.yo[:, CD * q:CD * q + CD]), "yst", 16)
+    need("y", Y, ("yst", 64))
+    need("g", g, ("snt", nsent))

@@ -7,22 +7,23 @@ WIN = 152
 KO = CAP // 4
 ND, CD, XC = 64, 16, 1024
 XA = 1408
-CUT = 16
+CUT = (18, 8, 8, 18)
 LOW = -1.0e29
-HOLD = 8192
+H = 2048
+W0 = 64
 
 F, I, U, B = "float32", "int32", "uint16", "bfloat16"
 SCRATCH = {n: ("sbuf", [128, w], d) for n, w, d in [
-    ("xw", 4 * (XC + CAP), B), ("qt", 512, B), ("tile", 16 * CAP, B),
+    ("xw", 4 * XC, B), ("qt", 512, B), ("tile", 16 * CAP, B),
     ("qwc", 128, "float8_e4m3fn_x4"), ("qws", 128, "uint8"), ("qc", 4 * CAP, "float8_e4m3fn_x4"), ("qs", 4 * CAP, "uint8"),
     ("lc", 3 * CAP, "float8_e4m3fn_x4"), ("lp", 3 * CAP, "uint8"),
-    ("cdl", 4, I), ("cds", 4, U), ("lst", 12, U), ("lo", 4, U),
-    ("row", 128, I), ("bc", 128, I), ("stw", 64, F), ("lnw", 64, F), ("nl", 64, F), ("nen", 64, F),
-    ("MG", 64, F), ("C", 64, F), ("ST", 72, F), ("J", 64, F), ("cL", 8, U), ("seL", 6, U),
-    ("D", 4 * WIN, F), ("SS", 4 * CAP, F), ("XX", 4 * CAP, F), ("O", CAP, U),
-    ("mask", 4 * WIN, F), ("Z", 4 * WIN, F), ("yo", 64, F), ("neg", 16, F),
-    ("lrow", 96, F), ("lcol", 96, F), ("u16", 64, F), ("u4", CAP, F), ("pc", 8, F), ("po", 8, U),
-    ("tri", 64, F), ("resm", 64, F), ("A", CAP, F), ("four", CAP, F)]}
+    ("cdl", 4, I), ("cds", 4, U), ("lst", 12, U), ("lo", 8, U),
+    ("row", 128, I), ("bc", 128, I), ("tab", 128, F), ("end", 64, F),
+    ("MG", 64, F), ("C", 64, F), ("J", 64, F), ("cL", 8, U), ("seL", 8, U),
+    ("D", W0 + 4 * WIN, F), ("SS", 4 * CAP, F), ("XX", 4 * CAP, F), ("O", CAP, U),
+    ("mask", 4 * WIN, F), ("yo", 64, F), ("neg", 48, F),
+    ("lrow", 64, F), ("lcol", 64, F), ("u16", 64, F), ("u4", CAP, F), ("pc", 8, F), ("po", 8, U),
+    ("tri", 64, F), ("step", 64, F), ("A", CAP, F), ("lim", CAP, F)]}
 SCRATCH["ps"] = ("psum", [128, 2048], F)
 SEMAPHORES = ["ldcd", "ldtab", "ldqw", "ldxa", "ldxb", "v", "s", "pe", "gi", "go", "lst", "sel",
               "arr0", "arr1", "arr2", "snt", "yst"]
@@ -39,7 +40,7 @@ def rank_program(g, core, T, topo):
     if rank is None:
         return
     V, S, P, Y = g.vector, g.scalar, g.tensor, g.sync
-    Copy = ActivationFunctionType.Copy
+    Copy, Identity = ActivationFunctionType.Copy, ActivationFunctionType.Identity
     chips = [topo.chip(c) for c in T.cores]
     steps = sorted([1, 3, 2], key=lambda v: 1 if topo.same_plane(chips[0], chips[v]) else 0)
     part = [rank ^ v for v in steps]
@@ -65,8 +66,14 @@ def rank_program(g, core, T, topo):
     def vneed(*toks):
         need("v", V, *toks)
 
+    def sneed(*toks):
+        need("s", S, *toks)
+
     def v(ins):
         return done(ins, "v")
+
+    def sc(ins):
+        return done(ins, "s")
 
     for k in range(8):
         q = Y if k < 4 else S
@@ -83,26 +90,26 @@ def rank_program(g, core, T, topo):
         return done(g.iota(out, pattern, base, 0, allow_small_or_imprecise_dtypes=True), "gi")
 
     iota(T.lrow[:, 0:32], [[0, 2], [4, 16]])
-    iota(T.lrow[:, 32:64], [[0, 2], [2 * HOLD, 4], [0, 4]])
-    i_row = iota(T.lrow[:, 64:96], [[0, 2], [-HOLD, 4], [-1, 4]], 3 * HOLD)
-    i_u16 = iota(T.u16[:], [[0, 4], [4, 16]])
+    i_row = iota(T.lrow[:, 32:64], [[0, 2], [-4 * H, 4], [1, 4]], 12 * H - 8)
     i_pc = iota(T.pc[:], [[64, 2], [1, 4]])
-    i_u4 = iota(T.u4[:], [[0, KO], [2 * HOLD, 4]], -HOLD)
-    lane4, turn, sub = T.lcol[:, 0:1], T.lcol[:, 32:33], T.lcol[:, 64:65]
+    i_u16 = iota(T.u16[:], [[0, 4], [4, 16]])
+    i_u4 = iota(T.u4[:], [[0, KO], [9 * H, 2], [5 * H, 2]], 8 - 16 * H)
+    lane4, turn = T.lcol[:, 0:1], T.lcol[:, 32:33]
 
-    v(V.memset(T.D[:], 0.0))
-    v(V.memset(T.xw[:, 4 * XC:4 * (XC + CAP)], 0.0))
-    v(V.memset(T.ST[:, 64:72], 0.0))
+    t_d = v(V.memset(T.D[:, W0:W0 + 4 * WIN], -1.0))
     vneed(i_row)
     t = v(V.transpose(T.lcol[:], T.lrow[:]))
-    v(V.memset(T.four[:], 4.0))
-    vneed(t, i_u16)
-    v(V.tensor_scalar(T.tri[:], T.u16[:], lane4, None, AluOpType.is_le))
-    v(V.tensor_scalar(T.resm[:], T.u16[:], 0.0, None, AluOpType.is_gt))
-    vneed(i_pc)
+    vneed(t, i_pc)
     t_po = v(V.tensor_scalar(T.po[:], T.pc[:], lane4, None, ADD))
+    vneed(i_u16)
+    v(V.tensor_scalar(T.tri[:], T.u16[:], lane4, None, AluOpType.is_le))
     vneed(i_u4)
-    t_a = v(V.tensor_scalar(T.A[:], T.u4[:], turn, float(HOLD), SUB, MIN))
+    v(V.tensor_scalar(T.A[:], T.u4[:], turn, float(H), ADD, MIN))
+
+    sneed(t_d)
+    sc(S.activation(T.lim[:], T.D[:, W0:W0 + CAP], Identity, bias=-float(XC + 1), scale=0.0))
+    sc(S.activation(T.neg[:], T.D[:, W0:W0 + 48], Identity, bias=LOW, scale=0.0))
+    t_fill = sc(S.activation(T.mask[:], T.D[:, W0:W0 + 4 * WIN], Copy, scale=0.0))
 
     vneed(t_cd)
     t = v(V.tensor_copy(T.cds[:], T.cdl[:]))
@@ -113,70 +120,66 @@ def rank_program(g, core, T, topo):
     g.sem_inc(T.sem.go, 1)
     need("g", g, t_tab)
     i_bc = done(g.partition_broadcast(T.bc[:], T.row[0:1, :], 128), "gi")
+    i_step = iota(T.step[:], [[WIN, 4], [0, 16]])
 
-    v(V.tensor_copy(T.lo[:, 3:4], T.cdl[:, rank:rank + 1]))
-    vneed(t_a)
-    t_const = v(V.memset(T.A[:, 0:CAP:4], -8.0 * HOLD))
-    v(V.memset(T.mask[:], 0.0))
-    v(V.memset(T.neg[:], LOW))
-    t_z = v(V.memset(T.Z[:, 0:4 * WIN:WIN], 0.0))
-
+    v(V.tensor_copy(T.lo[:, 0:1], T.cdl[:, rank:rank + 1]))
     vneed(i_bc, t_po)
-    t_ln = v(V.tensor_copy(T.lnw[:], T.bc[:].indirect(T.po[:, 4:8])))
-    t_stw = v(V.tensor_scalar(T.stw[:], T.bc[:].indirect(T.po[:, 0:4]), 4.0, -4.0, MUL, ADD))
-    vneed(t_ln)
-    t = v(V.tensor_scalar(T.nl[:], T.lnw[:], -4.0, None, MUL))
-    vneed(t_stw, t)
-    t_nen = v(V.tensor_tensor(T.nen[:], T.nl[:], T.stw[:], SUB))
+    t_t = v(V.tensor_copy(T.tab[:], T.bc[:].indirect(T.po[:])))
+    vneed(t_t)
+    t_end = v(V.tensor_tensor(T.end[:], T.tab[:, 0:64], T.tab[:, 64:128], ADD))
+    stw, lnw = T.tab[:, 0:64], T.tab[:, 64:128]
+
+    def win(buf, n, base=0):
+        return buf[:, base:base + WIN * (n - 1) + CAP + 1]
 
     vneed(("lst", 3 * ne))
-    t_lo = v(V.tensor_copy(T.lo[:, 0:3], T.lst[:, rank:12:4]))
-    need("s", S, t_lo)
-    t_st = done(S.activation(T.ST[:, 0:64], T.stw[:].indirect(T.lo[:]), Copy), "s")
+    t_lo = v(V.tensor_copy(T.lo[:, 1:4], T.lst[:, rank:12:4]))
+    lo = T.lo[:, 0:4]
+    sneed(t_lo, t_t)
+    t_st = sc(S.activation(T.D[:, 0:64], stw.indirect(lo), Identity, bias=-1.0, scale=-1.0))
     vneed(t_lo)
-    t = v(V.tensor_tensor(T.MG[:], T.lnw[:].indirect(T.lo[:]), T.tri[:], MUL))
+    t = v(V.tensor_tensor(T.MG[:], lnw.indirect(lo), T.tri[:], MUL))
+    vneed(t, i_step)
+    t = v(V.tensor_tensor_scan(T.C[:], T.step[:], T.MG[:], 0.0, MAX, ADD))
+    vneed(t_st, t_end)
+    v(V.tensor_tensor(T.J[:], T.end[:].indirect(lo), T.D[:, 1:65], ADD))
     vneed(t)
-    t = v(V.tensor_tensor_scan(T.C[:], T.resm[:], T.MG[:], 0.0, MUL, ADD))
-    vneed(t_st, t_nen)
-    v(V.tensor_tensor(T.J[:], T.nen[:].indirect(T.lo[:]), T.ST[:, 1:65], ADD))
-    vneed(t)
-    t_c = v(V.tensor_copy(T.cL[:, 0:8:2], T.C[:, 15:64:16]))
+    t_c = v(V.tensor_copy(T.cL[:, 0:4], T.C[:, 15:64:16]))
+    vneed(t_c, t_fill)
+    t_j = v(V.tensor_copy(win(T.D, 4, W0).indirect(T.cL[:, 0:4]), T.J[:]))
+    own_ends = T.cL[:, 0:1]
 
     need("g", g, t_c)
     share = [both[:h], both[h:h + h // 2], both[h + h // 2:]]
     g.remote_dma_fused([RemoteDMATransfer(dst_ids=[dsts[s]], dma_engine_mask=bits(share[s]), remote_sem=T.sem.sel,
-                                          srcs=[T.cL[:, 2 * s:2 * s + 1]], dsts=[T.seL[:, 2 * s:2 * s + 1]])
+                                          srcs=[T.cL[:, s + 1:s + 2]], dsts=[T.seL[:, s:s + 1]])
                         for s in range(3)], local_sem=T.sem.snt)
     nsent += ne
 
-    def jumps(k):
-        vneed(t_c)
-        return v(V.tensor_copy(T.D[:, WIN * k:WIN * k + CAP + 1].indirect(T.cL[:, 2 * k:2 * k + 1]), T.J[:, 16 * k:16 * k + 16]))
-
-    def run(k, t):
-        vneed(t)
-        return v(V.tensor_tensor_scan(T.SS[:, CAP * k:CAP * k + CAP], T.four[:], T.D[:, WIN * k:WIN * k + CAP],
-                                      T.ST[:, 16 * k:16 * k + 1], ADD, ADD))
+    def run(k):
+        vneed(t_j)
+        return v(V.tensor_tensor_scan(T.SS[:, CAP * k:CAP * k + CAP], T.D[:, W0 + WIN * k:W0 + WIN * k + CAP], T.lim[:],
+                                      T.D[:, 16 * k:16 * k + 1], ADD, MAX))
 
     def hold(k, t):
         vneed(t)
         return v(V.tensor_tensor_scan(T.XX[:, CAP * k:CAP * k + CAP], T.A[:], T.SS[:, CAP * k:CAP * k + CAP], 0.0, ADD, MAX))
 
-    def offsets(k, t):
+    def offsets(a, b, t):
         vneed(t)
-        return v(V.tensor_scalar(T.O[:, KO * k:KO * k + KO], T.XX[:, CAP * k + 3:CAP * k + CAP:4], sub, None, SUB))
+        return v(V.tensor_scalar(T.O[:, KO * a:KO * b], T.XX[:, CAP * a + 3:CAP * b:4], -4.0, turn, MUL, ADD))
 
     def piece(k, a, b):
         return (T.tile[:, 4 * CAP * k + 16 * a:4 * CAP * k + 16 * b], T.xw[:].indirect(T.O[:, KO * k + a:KO * k + b]))
 
     def gather_s(k, t_o):
-        need("s", S, t_o, t_xa, t_xb)
-        o, i = piece(k, CUT, KO)
-        return done(S.activation(o, i, Copy), "s")
+        sneed(t_o, t_xa, t_xb)
+        o, i = piece(k, CUT[k], KO)
+        return sc(S.activation(o, i, Copy))
 
     def gather_v(k, t_o):
         vneed(t_o, t_xa, t_xb)
-        o, i = piece(k, 0, CUT)
+        o, i = piece(k, 0, CUT[k])
         return v(V.tensor_copy(o, i))
 
     def quant(k, *toks):
@@ -184,80 +187,79 @@ def rank_program(g, core, T, topo):
         return v(V.quantize_mx(T.qc[:, CAP * k:CAP * k + CAP], T.qs[:, CAP * k:CAP * k + CAP],
                                T.tile[:, 4 * CAP * k:4 * CAP * (k + 1)]))
 
+    def codes(s):
+        return T.lc[:, CAP * s:CAP * s + CAP], T.qc[:, CAP * (s + 1):CAP * (s + 2)]
+
+    def plane(s):
+        return T.lp[:, CAP * s:CAP * s + CAP], T.qs[:, CAP * (s + 1):CAP * (s + 2)]
+
     def send_codes(s, t):
         need("g", g, t)
-        lo, hi = CAP * s, CAP * s + CAP
-        g.remote_dma(T.lc[:, lo:hi].bitcast(dt.uint8), T.qc[:, lo:hi].bitcast(dt.uint8), T.sem["arr%d" % s], T.sem.snt,
-                     addr[s][1], addr[s][0], bits(both))
+        o, i = codes(s)
+        g.remote_dma(o.bitcast(dt.uint8), i.bitcast(dt.uint8), T.sem["arr%d" % s], T.sem.snt, addr[s][1], addr[s][0], bits(both))
         return ne
 
-    a0 = jumps(0)
-    a1 = jumps(1)
-    b0 = run(0, a0)
-    a2 = jumps(2)
-    c0 = hold(0, b0)
-    b1 = run(1, a1)
-    o0 = offsets(0, c0)
+    b1 = run(1)
+    b2 = run(2)
     c1 = hold(1, b1)
-    b2 = run(2, a2)
-    o1 = offsets(1, c1)
     c2 = hold(2, b2)
-    s0 = gather_s(0, o0)
-    s1 = gather_s(1, o1)
-    o2 = offsets(2, c2)
-    s2 = gather_s(2, o2)
-    v0 = gather_v(0, o0)
-    nsent += send_codes(0, quant(0, v0, s0))
-    v1 = gather_v(1, o1)
-    nsent += send_codes(1, quant(1, v1, s1))
+    b3 = run(3)
+    o12 = offsets(1, 3, c2)
+    s1 = gather_s(1, o12)
+    s2 = gather_s(2, o12)
+    c3 = hold(3, b3)
+    v1 = gather_v(1, o12)
+    o3 = offsets(3, 4, c3)
+    s3 = gather_s(3, o3)
+    nsent += send_codes(0, quant(1, v1, s1))
+    v2 = gather_v(2, o12)
+    nsent += send_codes(1, quant(2, v2, s2))
     g.remote_dma_fused([RemoteDMATransfer(dst_ids=[dsts[s]], dma_engine_mask=bits(both[h * s:h * s + h]),
-                                          remote_sem=T.sem["arr%d" % s], srcs=[T.qs[:, CAP * s:CAP * s + CAP]],
-                                          dsts=[T.lp[:, CAP * s:CAP * s + CAP]]) for s in range(2)], local_sem=T.sem.snt)
+                                          remote_sem=T.sem["arr%d" % s], srcs=[plane(s)[1]], dsts=[plane(s)[0]])
+                        for s in range(2)], local_sem=T.sem.snt)
     nsent += ne
-    v2 = gather_v(2, o2)
-    nsent += send_codes(2, quant(2, v2, s2))
-    g.remote_dma(T.lp[:, 2 * CAP:3 * CAP], T.qs[:, 2 * CAP:3 * CAP], T.sem.arr2, T.sem.snt, addr[2][1], addr[2][0], bits(both))
+    v3 = gather_v(3, o3)
+    nsent += send_codes(2, quant(3, v3, s3))
+    g.remote_dma(plane(2)[0], plane(2)[1], T.sem.arr2, T.sem.snt, addr[2][1], addr[2][0], bits(both))
     nsent += ne
     n_arr = [ne + h, ne + h, 2 * ne]
 
-    def ends(k):
-        return T.cL[:, 6:7] if k == 3 else T.seL[:, 2 * k:2 * k + 1]
-
-    def marks(k):
-        vneed(t_z)
-        return v(V.tensor_copy(T.mask[:, WIN * k:WIN * k + CAP + 1].indirect(ends(k)), T.neg[:]))
-
-    t_mk = {}
-    a3 = jumps(3)
-    t_mk[3] = marks(3)
-    b3 = run(3, a3)
+    b0 = run(0)
+    v(V.tensor_copy(win(T.mask, 1).indirect(own_ends), T.neg[:, 0:16]))
+    c0 = hold(0, b0)
     vneed(t_qw)
     t_q = v(V.quantize_mx(T.qwc[:], T.qws[:], T.qt[:]))
-    c3 = hold(3, b3)
+    o0 = offsets(0, 1, c0)
+    s0 = gather_s(0, o0)
     vneed(("sel", ne))
-    t_mk[0] = marks(0)
-    o3 = offsets(3, c3)
-    t_mk[1] = marks(1)
-    s3 = gather_s(3, o3)
-    v3 = gather_v(3, o3)
-    t_mk[2] = marks(2)
-    t_q3 = quant(3, v3, s3)
+    t_mk = v(V.tensor_copy(win(T.mask, 4).indirect(T.seL[:, 0:3]), T.neg[:]))
+    t_q0 = quant(0, gather_v(0, o0), s0)
 
-    need("p", P, t_q)
-    for k in (3, 0, 1, 2):
-        if k == 3:
-            need("p", P, t_q3)
-            rc, rp, q = T.qc[:, 3 * CAP:4 * CAP], T.qs[:, 3 * CAP:4 * CAP], rank
+    def product(k):
+        if k == 0:
+            need("p", P, t_q, t_q0)
+            rc, rp = T.qc[:, 0:CAP], T.qs[:, 0:CAP]
         else:
-            need("p", P, ("arr%d" % k, n_arr[k]))
-            rc, rp, q = T.lc[:, CAP * k:CAP * k + CAP], T.lp[:, CAP * k:CAP * k + CAP], part[k]
+            need("p", P, ("arr%d" % (k - 1), n_arr[k - 1]))
+            rc, rp = codes(k - 1)[0], plane(k - 1)[0]
         t = done(P.matmul_mx(T.ps[:, 512 * k:512 * k + CAP], T.qwc[:], T.qws[:], rc, rp, True, True), "pe")
-        vneed(t, t_mk[k])
-        t = v(V.tensor_tensor_scan(T.Z[:, WIN * k + 1:WIN * k + 1 + CAP], T.mask[:, WIN * k:WIN * k + CAP],
-                                   T.ps[:, 512 * k:512 * k + CAP], LOW, ADD, MAX))
+        vneed(t, t_mk)
+        z = W0 + WIN * k + 1
+        return v(V.tensor_tensor_scan(T.D[:, z:z + CAP], T.mask[:, WIN * k:WIN * k + CAP],
+                                      T.ps[:, 512 * k:512 * k + CAP], LOW, ADD, MAX))
+
+    def pick(a, b, ends, t):
         vneed(t)
-        t = v(V.tensor_copy(T.yo[:, CD * q:CD * q + CD], T.Z[:, WIN * k:WIN * k + CAP + 1].indirect(ends(k))))
+        t = v(V.tensor_copy(T.yo[:, CD * a:CD * b], win(T.D, b, W0).indirect(ends)))
         need("y", Y, t)
-        done(Y.dma_start(T.y[:, CD * q:CD * q + CD], T.yo[:, CD * q:CD * q + CD]), "yst", 16)
+        for k in range(a, b):
+            q = part[k - 1] if k else rank
+            done(Y.dma_start(T.y[:, CD * q:CD * q + CD], T.yo[:, CD * k:CD * k + CD]), "yst", 16)
+
+    z0 = product(0)
+    z1 = product(1)
+    pick(0, 1, own_ends, z0)
+    pick(1, 3, T.seL[:, 0:2], product(2))
+    pick(3, 4, T.seL[:, 2:3], product(3))
     need("y", Y, ("yst", 64))
     need("g", g, ("snt", nsent))

@@ -6,26 +6,29 @@ CAP = 144
 WIN = 152
 KO = CAP // 4
 ND, CD, XC = 64, 16, 1024
-XA = 1408
-CUT = (18, 8, 8, 18)
+XA = 1792
+CUT = (8, 12, 12, 10)
 LOW = -1.0e29
 H = 2048
-W0 = 64
+OWN = 1
+NA, NB, W0 = WIN, WIN + 32, WIN + 80
+ORDER = ("lA x0 gA y0 cA lB jA eA gB sA cB r0 jB eB h0 sB o0 "
+         "r2 r3 h2 v0 o2 h3 r1 q0 o3 v2 h1 q2 v3 w0 o1 q3 v1 m0 q1").split()
 
 F, I, U, B = "float32", "int32", "uint16", "bfloat16"
 SCRATCH = {n: ("sbuf", [128, w], d) for n, w, d in [
     ("xw", 4 * XC, B), ("qt", 512, B), ("tile", 16 * CAP, B),
     ("qwc", 128, "float8_e4m3fn_x4"), ("qws", 128, "uint8"), ("qc", 4 * CAP, "float8_e4m3fn_x4"), ("qs", 4 * CAP, "uint8"),
     ("lc", 3 * CAP, "float8_e4m3fn_x4"), ("lp", 3 * CAP, "uint8"),
-    ("cdl", 4, I), ("cds", 4, U), ("lst", 12, U), ("lo", 8, U),
+    ("cdl", 4, I), ("lst", 4, I), ("lo", 8, U),
     ("row", 128, I), ("bc", 128, I), ("tab", 128, F), ("end", 64, F),
     ("MG", 64, F), ("C", 64, F), ("J", 64, F), ("cL", 8, U), ("seL", 8, U),
     ("D", W0 + 4 * WIN, F), ("SS", 4 * CAP, F), ("XX", 4 * CAP, F), ("O", CAP, U),
-    ("mask", 4 * WIN, F), ("yo", 64, F), ("neg", 48, F),
-    ("lrow", 64, F), ("lcol", 64, F), ("u16", 64, F), ("u4", CAP, F), ("pc", 8, F), ("po", 8, U),
-    ("tri", 64, F), ("step", 64, F), ("A", CAP, F), ("lim", CAP, F)]}
+    ("mask", 4 * WIN, F), ("yo", 64, F), ("neg", 64, F),
+    ("lrow", 64, F), ("lcol", 64, F), ("u16", 48, F), ("u4", CAP, F), ("pc", 8, F), ("po", 8, U),
+    ("tri", 48, F), ("step", 64, F), ("A", CAP, F), ("lim", CAP, F)]}
 SCRATCH["ps"] = ("psum", [128, 2048], F)
-SEMAPHORES = ["ldcd", "ldtab", "ldqw", "ldxa", "ldxb", "v", "s", "pe", "gi", "go", "lst", "sel",
+SEMAPHORES = ["ldcd", "ldtab", "ldqw", "ldxa", "ldxb", "v", "s", "pe", "gi", "go", "lstA", "lstB", "sel",
               "arr0", "arr1", "arr2", "snt", "yst"]
 
 ADD, SUB, MUL, MAX, MIN = AluOpType.add, AluOpType.subtract, AluOpType.mult, AluOpType.max, AluOpType.min
@@ -49,6 +52,9 @@ def rank_program(g, core, T, topo):
     dsts = [DstId(rid=a[0], pnc=a[1]) for a in addr]
     both = [e for e in eng[0] if e in eng[1] and e in eng[2]]
     ne, h = len(both), len(both) // 2
+    share = [both[:h], both[h:h + h // 2], both[h + h // 2:]]
+    list_of = [0, 2, 3]
+    step_of = {k: s for s, k in enumerate(list_of)}
 
     cnt, seen = {}, {}
 
@@ -92,174 +98,182 @@ def rank_program(g, core, T, topo):
     iota(T.lrow[:, 0:32], [[0, 2], [4, 16]])
     i_row = iota(T.lrow[:, 32:64], [[0, 2], [-4 * H, 4], [1, 4]], 12 * H - 8)
     i_pc = iota(T.pc[:], [[64, 2], [1, 4]])
-    i_u16 = iota(T.u16[:], [[0, 4], [4, 16]])
-    i_u4 = iota(T.u4[:], [[0, KO], [9 * H, 2], [5 * H, 2]], 8 - 16 * H)
+    i_u16 = iota(T.u16[:], [[0, 3], [4, 16]])
     lane4, turn = T.lcol[:, 0:1], T.lcol[:, 32:33]
 
-    t_d = v(V.memset(T.D[:, W0:W0 + 4 * WIN], -1.0))
+    t_d = v(V.memset(T.D[:], -1.0))
     vneed(i_row)
     t = v(V.transpose(T.lcol[:], T.lrow[:]))
     vneed(t, i_pc)
     t_po = v(V.tensor_scalar(T.po[:], T.pc[:], lane4, None, ADD))
     vneed(i_u16)
     v(V.tensor_scalar(T.tri[:], T.u16[:], lane4, None, AluOpType.is_le))
-    vneed(i_u4)
-    v(V.tensor_scalar(T.A[:], T.u4[:], turn, float(H), ADD, MIN))
 
     sneed(t_d)
     sc(S.activation(T.lim[:], T.D[:, W0:W0 + CAP], Identity, bias=-float(XC + 1), scale=0.0))
-    sc(S.activation(T.neg[:], T.D[:, W0:W0 + 48], Identity, bias=LOW, scale=0.0))
+    sc(S.activation(T.neg[:], T.D[:, W0:W0 + 64], Identity, bias=LOW, scale=0.0))
     t_fill = sc(S.activation(T.mask[:], T.D[:, W0:W0 + 4 * WIN], Copy, scale=0.0))
 
-    vneed(t_cd)
-    t = v(V.tensor_copy(T.cds[:], T.cdl[:]))
-    need("g", g, t)
-    g.remote_dma_fused([RemoteDMATransfer(dst_ids=dsts, dma_engine_mask=bits(both), remote_sem=T.sem.lst, srcs=[T.cds[:]],
-                                          dsts=[T.lst[:, 4 * s:4 * s + 4] for s in range(3)])], local_sem=T.sem.snt)
-    nsent = ne
+    need("g", g, t_cd)
+    g.remote_dma(T.lst[:, 0:1], T.cdl[:, part[0]:part[0] + 1], T.sem.lstA, T.sem.snt, addr[0][1], addr[0][0], bits(both))
+    g.remote_dma_fused([RemoteDMATransfer(dst_ids=[dsts[s]], dma_engine_mask=bits(both[h * s - h:h * s]),
+                                          remote_sem=T.sem.lstB, srcs=[T.cdl[:, part[s]:part[s] + 1]],
+                                          dsts=[T.lst[:, s:s + 1]]) for s in (1, 2)], local_sem=T.sem.snt)
+    nsent = [2 * ne]
     g.sem_inc(T.sem.go, 1)
     need("g", g, t_tab)
     i_bc = done(g.partition_broadcast(T.bc[:], T.row[0:1, :], 128), "gi")
     i_step = iota(T.step[:], [[WIN, 4], [0, 16]])
+    i_u4 = iota(T.u4[:], [[0, KO], [9 * H, 2], [5 * H, 2]], 8 - 16 * H)
 
-    v(V.tensor_copy(T.lo[:, 0:1], T.cdl[:, rank:rank + 1]))
+    vneed(t_cd)
+    v(V.tensor_copy(T.lo[:, 2:3], T.cdl[:, rank:rank + 1]))
     vneed(i_bc, t_po)
     t_t = v(V.tensor_copy(T.tab[:], T.bc[:].indirect(T.po[:])))
-    vneed(t_t)
-    t_end = v(V.tensor_tensor(T.end[:], T.tab[:, 0:64], T.tab[:, 64:128], ADD))
     stw, lnw = T.tab[:, 0:64], T.tab[:, 64:128]
 
     def win(buf, n, base=0):
         return buf[:, base:base + WIN * (n - 1) + CAP + 1]
 
-    vneed(("lst", 3 * ne))
-    t_lo = v(V.tensor_copy(T.lo[:, 1:4], T.lst[:, rank:12:4]))
-    lo = T.lo[:, 0:4]
-    sneed(t_lo, t_t)
-    t_st = sc(S.activation(T.D[:, 0:64], stw.indirect(lo), Identity, bias=-1.0, scale=-1.0))
-    vneed(t_lo)
-    t = v(V.tensor_tensor(T.MG[:], lnw.indirect(lo), T.tri[:], MUL))
-    vneed(t, i_step)
-    t = v(V.tensor_tensor_scan(T.C[:], T.step[:], T.MG[:], 0.0, MAX, ADD))
-    vneed(t_st, t_end)
-    v(V.tensor_tensor(T.J[:], T.end[:].indirect(lo), T.D[:, 1:65], ADD))
-    vneed(t)
-    t_c = v(V.tensor_copy(T.cL[:, 0:4], T.C[:, 15:64:16]))
-    vneed(t_c, t_fill)
-    t_j = v(V.tensor_copy(win(T.D, 4, W0).indirect(T.cL[:, 0:4]), T.J[:]))
-    own_ends = T.cL[:, 0:1]
+    tk = {}
+    col = {"A": slice(0, 1), "B": slice(2, 5)}
+    doc = {"A": (0, 16), "B": (16, 64)}
+    start = {"A": NA, "B": NB}
 
-    need("g", g, t_c)
-    share = [both[:h], both[h:h + h // 2], both[h + h // 2:]]
-    g.remote_dma_fused([RemoteDMATransfer(dst_ids=[dsts[s]], dma_engine_mask=bits(share[s]), remote_sem=T.sem.sel,
-                                          srcs=[T.cL[:, s + 1:s + 2]], dsts=[T.seL[:, s:s + 1]])
-                        for s in range(3)], local_sem=T.sem.snt)
-    nsent += ne
+    def table_ends(k):
+        vneed(t_t)
+        return v(V.tensor_tensor(T.end[:], stw, lnw, ADD))
 
-    def run(k):
-        vneed(t_j)
-        return v(V.tensor_tensor_scan(T.SS[:, CAP * k:CAP * k + CAP], T.D[:, W0 + WIN * k:W0 + WIN * k + CAP], T.lim[:],
-                                      T.D[:, 16 * k:16 * k + 1], ADD, MAX))
+    def table_hold(k):
+        vneed(i_u4)
+        return v(V.tensor_scalar(T.A[:], T.u4[:], turn, float(H), ADD, MIN))
 
-    def hold(k, t):
-        vneed(t)
-        return v(V.tensor_tensor_scan(T.XX[:, CAP * k:CAP * k + CAP], T.A[:], T.SS[:, CAP * k:CAP * k + CAP], 0.0, ADD, MAX))
+    def listed(k):
+        a, b = doc[k]
+        vneed(("lst" + k, ne))
+        t = v(V.tensor_copy(T.lo[:, 0:1], T.lst[:, 0:1]) if k == "A" else V.tensor_copy(T.lo[:, 3:5], T.lst[:, 1:3]))
+        sneed(t, t_t)
+        tk["n", k] = sc(S.activation(T.D[:, start[k]:start[k] + b - a], stw.indirect(T.lo[:, col[k]]), Identity,
+                                     bias=-1.0, scale=-1.0))
+        return t
 
-    def offsets(a, b, t):
-        vneed(t)
-        return v(V.tensor_scalar(T.O[:, KO * a:KO * b], T.XX[:, CAP * a + 3:CAP * b:4], -4.0, turn, MUL, ADD))
+    def lengths(k):
+        a, b = doc[k]
+        vneed(tk["l", k])
+        return v(V.tensor_tensor(T.MG[:, a:b], lnw.indirect(T.lo[:, col[k]]), T.tri[:, 0:b - a], MUL))
+
+    def ends(k):
+        a, b = doc[k]
+        vneed(tk["g", k], i_step)
+        return v(V.tensor_tensor_scan(T.C[:, a:b], T.step[:, a:b], T.MG[:, a:b], 0.0, MAX, ADD))
+
+    def jumps(k):
+        a, b = doc[k]
+        vneed(tk["n", k], tk["x", 0])
+        return v(V.tensor_tensor(T.J[:, a:b], T.end[:].indirect(T.lo[:, col[k]]),
+                                 T.D[:, start[k] + 1:start[k] + 1 + b - a], ADD))
+
+    def end_offsets(k):
+        a, b = doc[k]
+        vneed(tk["c", k])
+        t = v(V.tensor_copy(T.cL[:, col[k]], T.C[:, a + 15:b:16]))
+        if k == "B":
+            need("g", g, t)
+            src = [T.cL[:, 0:1], T.cL[:, 3:4], T.cL[:, 4:5]]
+            g.remote_dma_fused([RemoteDMATransfer(dst_ids=[dsts[s]], dma_engine_mask=bits(share[s]), remote_sem=T.sem.sel,
+                                                  srcs=[src[s]], dsts=[T.seL[:, rank:rank + 1]])
+                                for s in range(3)], local_sem=T.sem.snt)
+            nsent[0] += ne
+            need("y", Y, t)
+            Y.dma_start(T.seL[:, rank:rank + 1], T.cL[:, 2:3]).then_inc(T.sem.sel, 16)
+        return t
+
+    def spread(k):
+        a, b = doc[k]
+        vneed(tk["e", k], tk["j", k], t_fill)
+        window = win(T.D, 1) if k == "A" else win(T.D, 4, W0)
+        return v(V.tensor_copy(window.indirect(T.cL[:, col[k]]), T.J[:, a:b]))
+
+    def codes(s):
+        k = list_of[s]
+        return T.lc[:, CAP * s:CAP * s + CAP], T.qc[:, CAP * k:CAP * k + CAP]
+
+    def plane(s):
+        k = list_of[s]
+        return T.lp[:, CAP * s:CAP * s + CAP], T.qs[:, CAP * k:CAP * k + CAP]
 
     def piece(k, a, b):
         return (T.tile[:, 4 * CAP * k + 16 * a:4 * CAP * k + 16 * b], T.xw[:].indirect(T.O[:, KO * k + a:KO * k + b]))
 
-    def gather_s(k, t_o):
-        sneed(t_o, t_xa, t_xb)
-        o, i = piece(k, CUT[k], KO)
-        return sc(S.activation(o, i, Copy))
+    def run(k):
+        vneed(tk["s", "B" if k else "A"])
+        w, first = (W0 + WIN * k, NB + 16 * (k - 1)) if k else (0, NA)
+        return v(V.tensor_tensor_scan(T.SS[:, CAP * k:CAP * k + CAP], T.D[:, w:w + CAP], T.lim[:],
+                                      T.D[:, first:first + 1], ADD, MAX))
 
-    def gather_v(k, t_o):
-        vneed(t_o, t_xa, t_xb)
+    def hold(k):
+        vneed(tk["r", k], tk["y", 0])
+        return v(V.tensor_tensor_scan(T.XX[:, CAP * k:CAP * k + CAP], T.A[:], T.SS[:, CAP * k:CAP * k + CAP], 0.0, ADD, MAX))
+
+    def offsets(k):
+        vneed(tk["h", k])
+        t = v(V.tensor_scalar(T.O[:, KO * k:KO * k + KO], T.XX[:, CAP * k + 3:CAP * k + CAP:4], -4.0, turn, MUL, ADD))
+        sneed(t, t_xa, t_xb)
+        o, i = piece(k, CUT[k], KO)
+        tk["z", k] = sc(S.activation(o, i, Copy))
+        return t
+
+    def gather(k):
+        vneed(tk["o", k], t_xa, t_xb)
         o, i = piece(k, 0, CUT[k])
         return v(V.tensor_copy(o, i))
 
-    def quant(k, *toks):
-        vneed(*toks)
-        return v(V.quantize_mx(T.qc[:, CAP * k:CAP * k + CAP], T.qs[:, CAP * k:CAP * k + CAP],
-                               T.tile[:, 4 * CAP * k:4 * CAP * (k + 1)]))
+    def quant(k):
+        vneed(tk["v", k], tk["z", k])
+        t = v(V.quantize_mx(T.qc[:, CAP * k:CAP * k + CAP], T.qs[:, CAP * k:CAP * k + CAP],
+                            T.tile[:, 4 * CAP * k:4 * CAP * (k + 1)]))
+        if k != OWN:
+            s = step_of[k]
+            need("g", g, t)
+            for o, i in ([a.bitcast(dt.uint8) for a in codes(s)], plane(s)):
+                g.remote_dma(o, i, T.sem["arr%d" % s], T.sem.snt, addr[s][1], addr[s][0], bits(both))
+            nsent[0] += 2 * ne
+        return t
 
-    def codes(s):
-        return T.lc[:, CAP * s:CAP * s + CAP], T.qc[:, CAP * (s + 1):CAP * (s + 2)]
+    def queries(k):
+        vneed(t_qw)
+        return v(V.quantize_mx(T.qwc[:], T.qws[:], T.qt[:]))
 
-    def plane(s):
-        return T.lp[:, CAP * s:CAP * s + CAP], T.qs[:, CAP * (s + 1):CAP * (s + 2)]
+    def marks(k):
+        vneed(("sel", ne + 16))
+        return v(V.tensor_copy(win(T.mask, 4).indirect(T.seL[:, 0:4]), T.neg[:]))
 
-    def send_codes(s, t):
-        need("g", g, t)
-        o, i = codes(s)
-        g.remote_dma(o.bitcast(dt.uint8), i.bitcast(dt.uint8), T.sem["arr%d" % s], T.sem.snt, addr[s][1], addr[s][0], bits(both))
-        return ne
-
-    b1 = run(1)
-    b2 = run(2)
-    c1 = hold(1, b1)
-    c2 = hold(2, b2)
-    b3 = run(3)
-    o12 = offsets(1, 3, c2)
-    s1 = gather_s(1, o12)
-    s2 = gather_s(2, o12)
-    c3 = hold(3, b3)
-    v1 = gather_v(1, o12)
-    o3 = offsets(3, 4, c3)
-    s3 = gather_s(3, o3)
-    nsent += send_codes(0, quant(1, v1, s1))
-    v2 = gather_v(2, o12)
-    nsent += send_codes(1, quant(2, v2, s2))
-    g.remote_dma_fused([RemoteDMATransfer(dst_ids=[dsts[s]], dma_engine_mask=bits(both[h * s:h * s + h]),
-                                          remote_sem=T.sem["arr%d" % s], srcs=[plane(s)[1]], dsts=[plane(s)[0]])
-                        for s in range(2)], local_sem=T.sem.snt)
-    nsent += ne
-    v3 = gather_v(3, o3)
-    nsent += send_codes(2, quant(3, v3, s3))
-    g.remote_dma(plane(2)[0], plane(2)[1], T.sem.arr2, T.sem.snt, addr[2][1], addr[2][0], bits(both))
-    nsent += ne
-    n_arr = [ne + h, ne + h, 2 * ne]
-
-    b0 = run(0)
-    v(V.tensor_copy(win(T.mask, 1).indirect(own_ends), T.neg[:, 0:16]))
-    c0 = hold(0, b0)
-    vneed(t_qw)
-    t_q = v(V.quantize_mx(T.qwc[:], T.qws[:], T.qt[:]))
-    o0 = offsets(0, 1, c0)
-    s0 = gather_s(0, o0)
-    vneed(("sel", ne))
-    t_mk = v(V.tensor_copy(win(T.mask, 4).indirect(T.seL[:, 0:3]), T.neg[:]))
-    t_q0 = quant(0, gather_v(0, o0), s0)
+    step = {"x": table_ends, "y": table_hold, "l": listed, "g": lengths, "c": ends, "j": jumps, "e": end_offsets,
+            "s": spread, "r": run, "h": hold, "o": offsets, "v": gather, "q": quant, "w": queries, "m": marks}
+    for name in ORDER:
+        k = name[1] if name[1] in doc else int(name[1])
+        tk[name[0], k] = step[name[0]](k)
 
     def product(k):
-        if k == 0:
-            need("p", P, t_q, t_q0)
-            rc, rp = T.qc[:, 0:CAP], T.qs[:, 0:CAP]
+        if k == OWN:
+            need("p", P, tk["w", 0], tk["q", k])
+            rc, rp = T.qc[:, CAP * k:CAP * k + CAP], T.qs[:, CAP * k:CAP * k + CAP]
         else:
-            need("p", P, ("arr%d" % (k - 1), n_arr[k - 1]))
-            rc, rp = codes(k - 1)[0], plane(k - 1)[0]
+            s = step_of[k]
+            need("p", P, tk["w", 0], ("arr%d" % s, 2 * ne))
+            rc, rp = codes(s)[0], plane(s)[0]
         t = done(P.matmul_mx(T.ps[:, 512 * k:512 * k + CAP], T.qwc[:], T.qws[:], rc, rp, True, True), "pe")
-        vneed(t, t_mk)
+        vneed(t, tk["m", 0])
         z = W0 + WIN * k + 1
         return v(V.tensor_tensor_scan(T.D[:, z:z + CAP], T.mask[:, WIN * k:WIN * k + CAP],
                                       T.ps[:, 512 * k:512 * k + CAP], LOW, ADD, MAX))
 
-    def pick(a, b, ends, t):
-        vneed(t)
-        t = v(V.tensor_copy(T.yo[:, CD * a:CD * b], win(T.D, b, W0).indirect(ends)))
+    for a in (0, 2):
+        product(a)
+        vneed(product(a + 1))
+        q = (part[a] // 2) * 2
+        t = v(V.tensor_copy(T.yo[:, CD * q:CD * q + 2 * CD], win(T.D, a + 2, W0).indirect(T.seL[:, q:q + 2])))
         need("y", Y, t)
-        for k in range(a, b):
-            q = part[k - 1] if k else rank
-            done(Y.dma_start(T.y[:, CD * q:CD * q + CD], T.yo[:, CD * k:CD * k + CD]), "yst", 16)
-
-    z0 = product(0)
-    z1 = product(1)
-    pick(0, 1, own_ends, z0)
-    pick(1, 3, T.seL[:, 0:2], product(2))
-    pick(3, 4, T.seL[:, 2:3], product(3))
-    need("y", Y, ("yst", 64))
-    need("g", g, ("snt", nsent))
+        done(Y.dma_start(T.y[:, CD * q:CD * q + 2 * CD], T.yo[:, CD * q:CD * q + 2 * CD]), "yst", 16)
+    need("y", Y, ("yst", 32))
+    need("g", g, ("snt", nsent[0]))

@@ -7,52 +7,89 @@ WIN = 152
 KO = CAP // 4
 ND, CD, XC = 64, 16, 1024
 XA = 1792
-CUT = (8, 12, 12, 10)
+CUT = ((10, 4), (20,), (4, 10), (12,))
 LOW = -1.0e29
 H = 2048
 OWN = 1
-NA, NB, W0 = WIN, WIN + 32, WIN + 80
-ORDER = ("lA x0 gA y0 cA lB jA eA gB sA cB r0 jB eB h0 sB o0 "
-         "r2 r3 h2 v0 o2 h3 r1 q0 o3 v2 h1 q2 v3 w0 o1 q3 v1 m0 q1").split()
+NA, NB, W0 = WIN, WIN + 24, WIN + 48
+ORDER = ("l0 x0 gA l2 l3 cA jA gB eA y0 cB sA jB eB rA sB hA rB o0 hB "
+         "v0 o2 v0 o3 v2 q0 v2 o1 q2 v3 w0 q3 v1 q1 m0").split()
 
 F, I, U, B = "float32", "int32", "uint16", "bfloat16"
 SCRATCH = {n: ("sbuf", [128, w], d) for n, w, d in [
     ("xw", 4 * XC, B), ("qt", 512, B), ("tile", 16 * CAP, B),
     ("qwc", 128, "float8_e4m3fn_x4"), ("qws", 128, "uint8"), ("qc", 4 * CAP, "float8_e4m3fn_x4"), ("qs", 4 * CAP, "uint8"),
     ("lc", 3 * CAP, "float8_e4m3fn_x4"), ("lp", 3 * CAP, "uint8"),
-    ("cdl", 4, I), ("lst", 4, I), ("lo", 8, U),
+    ("cdl", 4, I), ("lst", 4, I), ("lo", 4, U),
     ("row", 128, I), ("bc", 128, I), ("tab", 128, F), ("end", 64, F),
-    ("MG", 64, F), ("C", 64, F), ("J", 64, F), ("cL", 8, U), ("seL", 8, U),
-    ("D", W0 + 4 * WIN, F), ("SS", 4 * CAP, F), ("XX", 4 * CAP, F), ("O", CAP, U),
+    ("MG", 32, F), ("C", 32, F), ("J", 32, F), ("cL", 4, U), ("cS", 16, U), ("seL", 8, U),
+    ("D", W0 + 4 * WIN, F), ("SS", 2 * CAP, F), ("XX", 2 * CAP, F), ("O", CAP, U),
     ("mask", 4 * WIN, F), ("yo", 64, F), ("neg", 64, F),
-    ("lrow", 64, F), ("lcol", 64, F), ("u16", 48, F), ("u4", CAP, F), ("pc", 8, F), ("po", 8, U),
-    ("tri", 48, F), ("step", 64, F), ("A", CAP, F), ("lim", CAP, F)]}
+    ("lrow", 64, F), ("lcol", 64, F), ("u16", 16, F), ("u4", CAP, F), ("pc", 8, F), ("po", 8, U),
+    ("tri", 16, F), ("A", CAP, F), ("lim", CAP, F)]}
 SCRATCH["ps"] = ("psum", [128, 2048], F)
-SEMAPHORES = ["ldcd", "ldtab", "ldqw", "ldxa", "ldxb", "v", "s", "pe", "gi", "go", "lstA", "lstB", "sel",
+SEMAPHORES = ["ldcd", "ldtab", "ldqw", "ldxa", "ldxb", "v", "s", "pe", "gi", "go", "lstA", "lstB", "sel", "hendsA", "hendsB", "hplane",
               "arr0", "arr1", "arr2", "snt", "yst"]
 
 ADD, SUB, MUL, MAX, MIN = AluOpType.add, AluOpType.subtract, AluOpType.mult, AluOpType.max, AluOpType.min
+HALF = (slice(0, 64), slice(64, 128))
 
 
 def bits(engines):
     return sum(1 << e for e in engines)
 
 
-def rank_program(g, core, T, topo):
-    rank = T.rank_of(core)
-    if rank is None:
-        return
-    V, S, P, Y = g.vector, g.scalar, g.tensor, g.sync
-    Copy, Identity = ActivationFunctionType.Copy, ActivationFunctionType.Identity
+def helper_of(core, T, topo):
+    return [c for c in topo.cores_of(core) if topo.die(c) != topo.die(core)
+            and all(topo.may_write(c, d) for d in T.cores)][0]
+
+
+def partners(rank, core, T, topo):
     chips = [topo.chip(c) for c in T.cores]
     steps = sorted([1, 3, 2], key=lambda v: 1 if topo.same_plane(chips[0], chips[v]) else 0)
     part = [rank ^ v for v in steps]
     addr = [topo.addr(T.cores[p]) for p in part]
     eng = [topo.engines(core, T.cores[p]) for p in part]
-    dsts = [DstId(rid=a[0], pnc=a[1]) for a in addr]
-    both = [e for e in eng[0] if e in eng[1] and e in eng[2]]
+    return part, addr, [e for e in eng[0] if e in eng[1] and e in eng[2]]
+
+
+def helper_program(g, core, rank, T, topo):
+    part, addr, both = partners(rank, core, T, topo)
     ne, h = len(both), len(both) // 2
-    share = [both[:h], both[h:h + h // 2], both[h + h // 2:]]
+    home = topo.addr(T.cores[rank])
+    near = [e for e in topo.engines(core, T.cores[rank]) if e not in both]
+    who = [addr[0], home, addr[1], addr[2]]
+    for u in range(2):
+        g.vector.wait_ge(T.sem["hends" + "AB"[u]], len(near))
+        for src in range(2):
+            for out in HALF:
+                g.vector.tensor_scalar(T.cS[out, 8 * u + src:8 * u + src + 1], T.cL[HALF[src], 2 * u:2 * u + 1],
+                                       float(WIN * src), None, ADD).then_inc(T.sem.v, 1)
+        g.wait_ge(T.sem.v, 4 * u + 4)
+        g.remote_dma_fused(
+            [RemoteDMATransfer(dst_ids=[DstId(rid=who[2 * u + j][0], pnc=who[2 * u + j][1])],
+                               dma_engine_mask=bits(both[h * j:h * j + h]), remote_sem=T.sem.sel,
+                               srcs=[T.cS[:, 8 * u + j:8 * u + j + 1]], dsts=[T.seL[:, rank:rank + 1]])
+             for j in range(2)], local_sem=T.sem.snt)
+    g.wait_ge(T.sem.hplane, len(near))
+    g.remote_dma(T.lp[:, 0:CAP], T.lp[:, 0:CAP], T.sem.arr0, T.sem.snt, addr[0][1], addr[0][0], bits(both))
+    g.wait_ge(T.sem.snt, 3 * ne)
+
+
+def rank_program(g, core, T, topo):
+    rank = T.rank_of(core)
+    if rank is None:
+        for r, c in enumerate(T.cores):
+            if helper_of(c, T, topo) == core:
+                helper_program(g, core, r, T, topo)
+        return
+    V, S, P, Y = g.vector, g.scalar, g.tensor, g.sync
+    Copy, Identity = ActivationFunctionType.Copy, ActivationFunctionType.Identity
+    part, addr, both = partners(rank, core, T, topo)
+    dsts = [DstId(rid=a[0], pnc=a[1]) for a in addr]
+    ne, h = len(both), len(both) // 2
+    helper = topo.addr(helper_of(core, T, topo))
+    near = [e for e in topo.engines(core, helper_of(core, T, topo)) if e not in both]
     list_of = [0, 2, 3]
     step_of = {k: s for s, k in enumerate(list_of)}
 
@@ -81,12 +118,12 @@ def rank_program(g, core, T, topo):
     def sc(ins):
         return done(ins, "s")
 
-    for k in range(8):
-        q = Y if k < 4 else S
+    for k in range(4):
+        q = Y if k < 2 else S
         done(q.dma_start(T.cdl[16 * k:16 * k + 16, :], T.cd[:]), "ldcd", 16)
     done(S.dma_start(T.row[0:1, 0:64], T.st[:]), "ldtab", 16)
     done(S.dma_start(T.row[0:1, 64:128], T.ln[:]), "ldtab", 16)
-    t_cd, t_tab = ("ldcd", 128), ("ldtab", 32)
+    t_cd, t_tab = ("ldcd", 64), ("ldtab", 32)
     t_xa = done(Y.dma_start(T.xw[:, 0:XA], T.x[:, 0:XA]), "ldxa", 16)
     Y.wait_ge(T.sem.go, 1)
     t_xb = done(Y.dma_start(T.xw[:, XA:4 * XC], T.x[:, XA:4 * XC]), "ldxb", 16)
@@ -98,9 +135,10 @@ def rank_program(g, core, T, topo):
     iota(T.lrow[:, 0:32], [[0, 2], [4, 16]])
     i_row = iota(T.lrow[:, 32:64], [[0, 2], [-4 * H, 4], [1, 4]], 12 * H - 8)
     i_pc = iota(T.pc[:], [[64, 2], [1, 4]])
-    i_u16 = iota(T.u16[:], [[0, 3], [4, 16]])
+    i_u16 = iota(T.u16[:], [[4, 16]])
     lane4, turn = T.lcol[:, 0:1], T.lcol[:, 32:33]
 
+    t_0 = v(V.memset(T.cdl[HALF[1], :], 0))
     t_d = v(V.memset(T.D[:], -1.0))
     vneed(i_row)
     t = v(V.transpose(T.lcol[:], T.lrow[:]))
@@ -114,7 +152,7 @@ def rank_program(g, core, T, topo):
     sc(S.activation(T.neg[:], T.D[:, W0:W0 + 64], Identity, bias=LOW, scale=0.0))
     t_fill = sc(S.activation(T.mask[:], T.D[:, W0:W0 + 4 * WIN], Copy, scale=0.0))
 
-    need("g", g, t_cd)
+    need("g", g, t_0, t_cd)
     g.remote_dma(T.lst[:, 0:1], T.cdl[:, part[0]:part[0] + 1], T.sem.lstA, T.sem.snt, addr[0][1], addr[0][0], bits(both))
     g.remote_dma_fused([RemoteDMATransfer(dst_ids=[dsts[s]], dma_engine_mask=bits(both[h * s - h:h * s]),
                                           remote_sem=T.sem.lstB, srcs=[T.cdl[:, part[s]:part[s] + 1]],
@@ -123,11 +161,10 @@ def rank_program(g, core, T, topo):
     g.sem_inc(T.sem.go, 1)
     need("g", g, t_tab)
     i_bc = done(g.partition_broadcast(T.bc[:], T.row[0:1, :], 128), "gi")
-    i_step = iota(T.step[:], [[WIN, 4], [0, 16]])
     i_u4 = iota(T.u4[:], [[0, KO], [9 * H, 2], [5 * H, 2]], 8 - 16 * H)
 
     vneed(t_cd)
-    v(V.tensor_copy(T.lo[:, 2:3], T.cdl[:, rank:rank + 1]))
+    v(V.tensor_copy(T.lo[HALF[1], 0:1], T.cdl[HALF[0], rank:rank + 1]))
     vneed(i_bc, t_po)
     t_t = v(V.tensor_copy(T.tab[:], T.bc[:].indirect(T.po[:])))
     stw, lnw = T.tab[:, 0:64], T.tab[:, 64:128]
@@ -136,9 +173,17 @@ def rank_program(g, core, T, topo):
         return buf[:, base:base + WIN * (n - 1) + CAP + 1]
 
     tk = {}
-    col = {"A": slice(0, 1), "B": slice(2, 5)}
-    doc = {"A": (0, 16), "B": (16, 64)}
+    grp = {"A": 0, "B": 1}
     start = {"A": NA, "B": NB}
+
+    def col(buf, k):
+        return buf[:, 2 * grp[k]:2 * grp[k] + 1]
+
+    def doc(buf, k):
+        return buf[:, 16 * grp[k]:16 * grp[k] + 16]
+
+    def tok(buf, k):
+        return buf[:, CAP * grp[k]:CAP * grp[k] + CAP]
 
     def table_ends(k):
         vneed(t_t)
@@ -149,50 +194,49 @@ def rank_program(g, core, T, topo):
         return v(V.tensor_scalar(T.A[:], T.u4[:], turn, float(H), ADD, MIN))
 
     def listed(k):
-        a, b = doc[k]
-        vneed(("lst" + k, ne))
-        t = v(V.tensor_copy(T.lo[:, 0:1], T.lst[:, 0:1]) if k == "A" else V.tensor_copy(T.lo[:, 3:5], T.lst[:, 1:3]))
-        sneed(t, t_t)
-        tk["n", k] = sc(S.activation(T.D[:, start[k]:start[k] + b - a], stw.indirect(T.lo[:, col[k]]), Identity,
-                                     bias=-1.0, scale=-1.0))
+        u, s = "AB"[k // 2], step_of[k]
+        vneed(("lst" + u, ne))
+        t = v(V.tensor_copy(T.lo[HALF[k % 2], 2 * grp[u]:2 * grp[u] + 1], T.lst[HALF[0], s:s + 1]))
+        tk["l", u] = t
+        if k != 2:
+            sneed(t, t_t)
+            tk["n", u] = sc(S.activation(T.D[:, start[u]:start[u] + 16], stw.indirect(col(T.lo, u)), Identity,
+                                         bias=-1.0, scale=-1.0))
         return t
 
     def lengths(k):
-        a, b = doc[k]
         vneed(tk["l", k])
-        return v(V.tensor_tensor(T.MG[:, a:b], lnw.indirect(T.lo[:, col[k]]), T.tri[:, 0:b - a], MUL))
+        return v(V.tensor_tensor(doc(T.MG, k), lnw.indirect(col(T.lo, k)), T.tri[:], MUL))
 
     def ends(k):
-        a, b = doc[k]
-        vneed(tk["g", k], i_step)
-        return v(V.tensor_tensor_scan(T.C[:, a:b], T.step[:, a:b], T.MG[:, a:b], 0.0, MAX, ADD))
+        vneed(tk["g", k], t_fill)
+        return v(V.tensor_tensor_scan(doc(T.C, k), T.lim[:, 0:16], doc(T.MG, k), float(2 * WIN * grp[k]), MAX, ADD))
 
     def jumps(k):
-        a, b = doc[k]
         vneed(tk["n", k], tk["x", 0])
-        return v(V.tensor_tensor(T.J[:, a:b], T.end[:].indirect(T.lo[:, col[k]]),
-                                 T.D[:, start[k] + 1:start[k] + 1 + b - a], ADD))
+        return v(V.tensor_tensor(doc(T.J, k), T.end[:].indirect(col(T.lo, k)), T.D[:, start[k] + 1:start[k] + 17], ADD))
 
     def end_offsets(k):
-        a, b = doc[k]
         vneed(tk["c", k])
-        t = v(V.tensor_copy(T.cL[:, col[k]], T.C[:, a + 15:b:16]))
-        if k == "B":
-            need("g", g, t)
-            src = [T.cL[:, 0:1], T.cL[:, 3:4], T.cL[:, 4:5]]
-            g.remote_dma_fused([RemoteDMATransfer(dst_ids=[dsts[s]], dma_engine_mask=bits(share[s]), remote_sem=T.sem.sel,
-                                                  srcs=[src[s]], dsts=[T.seL[:, rank:rank + 1]])
-                                for s in range(3)], local_sem=T.sem.snt)
-            nsent[0] += ne
-            need("y", Y, t)
-            Y.dma_start(T.seL[:, rank:rank + 1], T.cL[:, 2:3]).then_inc(T.sem.sel, 16)
+        t = v(V.tensor_copy(col(T.cL, k), T.C[:, 16 * grp[k] + 15:16 * grp[k] + 16]))
+        need("g", g, t)
+        g.remote_dma(col(T.cL, k), col(T.cL, k), T.sem["hends" + k], T.sem.snt, helper[1], helper[0], bits(near))
+        nsent[0] += len(near)
         return t
 
     def spread(k):
-        a, b = doc[k]
-        vneed(tk["e", k], tk["j", k], t_fill)
-        window = win(T.D, 1) if k == "A" else win(T.D, 4, W0)
-        return v(V.tensor_copy(window.indirect(T.cL[:, col[k]]), T.J[:, a:b]))
+        vneed(tk["e", k], tk["j", k])
+        window = win(T.D, 1) if k == "A" else win(T.D, 3, W0)
+        return v(V.tensor_copy(window.indirect(col(T.cL, k)), doc(T.J, k)))
+
+    def run(k):
+        vneed(tk["s", k])
+        w = 0 if k == "A" else W0 + 2 * WIN
+        return v(V.tensor_tensor_scan(tok(T.SS, k), T.D[:, w:w + CAP], T.lim[:], T.D[:, start[k]:start[k] + 1], ADD, MAX))
+
+    def hold(k):
+        vneed(tk["r", k], tk["y", 0])
+        return v(V.tensor_tensor_scan(tok(T.XX, k), T.A[:], tok(T.SS, k), 0.0, ADD, MAX))
 
     def codes(s):
         k = list_of[s]
@@ -205,27 +249,24 @@ def rank_program(g, core, T, topo):
     def piece(k, a, b):
         return (T.tile[:, 4 * CAP * k + 16 * a:4 * CAP * k + 16 * b], T.xw[:].indirect(T.O[:, KO * k + a:KO * k + b]))
 
-    def run(k):
-        vneed(tk["s", "B" if k else "A"])
-        w, first = (W0 + WIN * k, NB + 16 * (k - 1)) if k else (0, NA)
-        return v(V.tensor_tensor_scan(T.SS[:, CAP * k:CAP * k + CAP], T.D[:, w:w + CAP], T.lim[:],
-                                      T.D[:, first:first + 1], ADD, MAX))
-
-    def hold(k):
-        vneed(tk["r", k], tk["y", 0])
-        return v(V.tensor_tensor_scan(T.XX[:, CAP * k:CAP * k + CAP], T.A[:], T.SS[:, CAP * k:CAP * k + CAP], 0.0, ADD, MAX))
-
     def offsets(k):
-        vneed(tk["h", k])
-        t = v(V.tensor_scalar(T.O[:, KO * k:KO * k + KO], T.XX[:, CAP * k + 3:CAP * k + CAP:4], -4.0, turn, MUL, ADD))
+        u, src = k // 2, HALF[k % 2]
+        vneed(tk["h", "AB"[u]])
+        for out in HALF:
+            t = v(V.tensor_scalar(T.O[out, KO * k:KO * k + KO], T.XX[src, CAP * u + 3:CAP * u + CAP:4], -4.0,
+                                  T.lcol[src, 32:33], MUL, ADD))
         sneed(t, t_xa, t_xb)
-        o, i = piece(k, CUT[k], KO)
+        o, i = piece(k, sum(CUT[k]), KO)
         tk["z", k] = sc(S.activation(o, i, Copy))
         return t
 
+    taken = [0] * 4
+
     def gather(k):
         vneed(tk["o", k], t_xa, t_xb)
-        o, i = piece(k, 0, CUT[k])
+        a = sum(CUT[k][:taken[k]])
+        o, i = piece(k, a, a + CUT[k][taken[k]])
+        taken[k] += 1
         return v(V.tensor_copy(o, i))
 
     def quant(k):
@@ -235,9 +276,14 @@ def rank_program(g, core, T, topo):
         if k != OWN:
             s = step_of[k]
             need("g", g, t)
-            for o, i in ([a.bitcast(dt.uint8) for a in codes(s)], plane(s)):
+            o, i = [a.bitcast(dt.uint8) for a in codes(s)]
+            g.remote_dma(o, i, T.sem["arr%d" % s], T.sem.snt, addr[s][1], addr[s][0], bits(both))
+            o, i = plane(s)
+            if s:
                 g.remote_dma(o, i, T.sem["arr%d" % s], T.sem.snt, addr[s][1], addr[s][0], bits(both))
-            nsent[0] += 2 * ne
+            else:
+                g.remote_dma(o, i, T.sem.hplane, T.sem.snt, helper[1], helper[0], bits(near))
+            nsent[0] += ne + (ne if s else len(near))
         return t
 
     def queries(k):
@@ -245,13 +291,14 @@ def rank_program(g, core, T, topo):
         return v(V.quantize_mx(T.qwc[:], T.qws[:], T.qt[:]))
 
     def marks(k):
-        vneed(("sel", ne + 16))
+        vneed(("sel", 2 * ne))
         return v(V.tensor_copy(win(T.mask, 4).indirect(T.seL[:, 0:4]), T.neg[:]))
 
     step = {"x": table_ends, "y": table_hold, "l": listed, "g": lengths, "c": ends, "j": jumps, "e": end_offsets,
-            "s": spread, "r": run, "h": hold, "o": offsets, "v": gather, "q": quant, "w": queries, "m": marks}
+            "s": spread, "r": run, "h": hold, "o": offsets, "v": gather, "q": quant,
+            "w": queries, "m": marks}
     for name in ORDER:
-        k = name[1] if name[1] in doc else int(name[1])
+        k = name[1] if name[1] in grp else int(name[1])
         tk[name[0], k] = step[name[0]](k)
 
     def product(k):
@@ -268,9 +315,9 @@ def rank_program(g, core, T, topo):
         return v(V.tensor_tensor_scan(T.D[:, z:z + CAP], T.mask[:, WIN * k:WIN * k + CAP],
                                       T.ps[:, 512 * k:512 * k + CAP], LOW, ADD, MAX))
 
+    z = {k: product(k) for k in (OWN, 2, 0, 3)}
     for a in (0, 2):
-        product(a)
-        vneed(product(a + 1))
+        vneed(z[a], z[a + 1])
         q = (part[a] // 2) * 2
         t = v(V.tensor_copy(T.yo[:, CD * q:CD * q + 2 * CD], win(T.D, a + 2, W0).indirect(T.seL[:, q:q + 2])))
         need("y", Y, t)

import numpy as np
from concourse.bass import DstId, RemoteDMATransfer
from concourse.mybir import dt, AluOpType, ActivationFunctionType

CAP = 144
WIN = 152
KO = CAP // 4
ND, CD, XC = 64, 16, 1024
XA = 1792
CUT = ((10, 4), (20,), (4, 10), (12,))
LOW = -1.0e29
H = 2048
OWN = 1
NA, NB, W0 = WIN, WIN + 24, WIN + 48
ORDER = ("l0 x0 gA l2 l3 cA jA gB eA y0 cB sA jB eB rA sB hA rB o0 hB "
         "v0 o2 v0 o3 v2 q0 v2 o1 q2 v3 w0 q3 v1 q1 m0").split()

F, I, U, B = "float32", "int32", "uint16", "bfloat16"
SCRATCH = {n: ("sbuf", [128, w], d) for n, w, d in [
    ("xw", 4 * XC, B), ("qt", 512, B), ("tile", 16 * CAP, B),
    ("qwc", 128, "float8_e4m3fn_x4"), ("qws", 128, "uint8"), ("qc", 4 * CAP, "float8_e4m3fn_x4"), ("qs", 4 * CAP, "uint8"),
    ("lc", 3 * CAP, "float8_e4m3fn_x4"), ("lp", 3 * CAP, "uint8"),
    ("cdl", 4, I), ("lst", 4, I), ("lo", 4, U),
    ("row", 128, I), ("bc", 128, I), ("tab", 128, F), ("end", 64, F),
    ("MG", 32, F), ("C", 32, F), ("J", 32, F), ("cL", 4, U), ("cS", 16, U), ("seL", 8, U),
    ("D", W0 + 4 * WIN, F), ("SS", 2 * CAP, F), ("XX", 2 * CAP, F), ("O", CAP, U),
    ("mask", 4 * WIN, F), ("yo", 64, F), ("neg", 64, F),
    ("lrow", 64, F), ("lcol", 64, F), ("u16", 16, F), ("u4", CAP, F), ("pc", 8, F), ("po", 8, U),
    ("tri", 16, F), ("A", CAP, F), ("lim", CAP, F)]}
SCRATCH["ps"] = ("psum", [128, 2048], F)
SEMAPHORES = ["ldcd", "ldtab", "ldqw", "ldxa", "ldxb", "v", "s", "pe", "gi", "go", "lstA", "lstB", "sel", "hendsA", "hendsB", "hplane",
              "arr0", "arr1", "arr2", "snt", "yst"]

ADD, SUB, MUL, MAX, MIN = AluOpType.add, AluOpType.subtract, AluOpType.mult, AluOpType.max, AluOpType.min
HALF = (slice(0, 64), slice(64, 128))


def bits(engines):
    return sum(1 << e for e in engines)


def helper_of(core, T, topo):
    return [c for c in topo.cores_of(core) if topo.die(c) != topo.die(core)
            and all(topo.may_write(c, d) for d in T.cores)][0]


def partners(rank, core, T, topo):
    chips = [topo.chip(c) for c in T.cores]
    steps = sorted([1, 3, 2], key=lambda v: 1 if topo.same_plane(chips[0], chips[v]) else 0)
    part = [rank ^ v for v in steps]
    addr = [topo.addr(T.cores[p]) for p in part]
    eng = [topo.engines(core, T.cores[p]) for p in part]
    return part, addr, [e for e in eng[0] if e in eng[1] and e in eng[2]]


def helper_program(g, core, rank, T, topo):
    part, addr, both = partners(rank, core, T, topo)
    ne, h = len(both), len(both) // 2
    home = topo.addr(T.cores[rank])
    near = [e for e in topo.engines(core, T.cores[rank]) if e not in both]
    who = [addr[0], home, addr[1], addr[2]]
    for u in range(2):
        g.vector.wait_ge(T.sem["hends" + "AB"[u]], len(near))
        for src in range(2):
            for out in HALF:
                g.vector.tensor_scalar(T.cS[out, 8 * u + src:8 * u + src + 1], T.cL[HALF[src], 2 * u:2 * u + 1],
                                       float(WIN * src), None, ADD).then_inc(T.sem.v, 1)
        g.wait_ge(T.sem.v, 4 * u + 4)
        g.remote_dma_fused(
            [RemoteDMATransfer(dst_ids=[DstId(rid=who[2 * u + j][0], pnc=who[2 * u + j][1])],
                               dma_engine_mask=bits(both[h * j:h * j + h]), remote_sem=T.sem.sel,
                               srcs=[T.cS[:, 8 * u + j:8 * u + j + 1]], dsts=[T.seL[:, rank:rank + 1]])
             for j in range(2)], local_sem=T.sem.snt)
    g.wait_ge(T.sem.hplane, len(near))
    g.remote_dma(T.lp[:, 0:CAP], T.lp[:, 0:CAP], T.sem.arr0, T.sem.snt, addr[0][1], addr[0][0], bits(both))
    g.wait_ge(T.sem.snt, 3 * ne)


def rank_program(g, core, T, topo):
    rank = T.rank_of(core)
    if rank is None:
        for r, c in enumerate(T.cores):
            if helper_of(c, T, topo) == core:
                helper_program(g, core, r, T, topo)
        return
    V, S, P, Y = g.vector, g.scalar, g.tensor, g.sync
    Copy, Identity = ActivationFunctionType.Copy, ActivationFunctionType.Identity
    part, addr, both = partners(rank, core, T, topo)
    dsts = [DstId(rid=a[0], pnc=a[1]) for a in addr]
    ne, h = len(both), len(both) // 2
    helper = topo.addr(helper_of(core, T, topo))
    near = [e for e in topo.engines(core, helper_of(core, T, topo)) if e not in both]
    list_of = [0, 2, 3]
    step_of = {k: s for s, k in enumerate(list_of)}

    cnt, seen = {}, {}

    def done(ins, name, n=1):
        ins.then_inc(T.sem[name], n)
        cnt[name] = cnt.get(name, 0) + n
        return (name, cnt[name])

    def need(qn, q, *toks):
        for name, val in toks:
            if seen.get((qn, name), 0) < val:
                q.wait_ge(T.sem[name], val)
                seen[(qn, name)] = val

    def vneed(*toks):
        need("v", V, *toks)

    def sneed(*toks):
        need("s", S, *toks)

    def v(ins):
        return done(ins, "v")

    def sc(ins):
        return done(ins, "s")

    for k in range(4):
        q = Y if k < 2 else S
        done(q.dma_start(T.cdl[16 * k:16 * k + 16, :], T.cd[:]), "ldcd", 16)
    done(S.dma_start(T.row[0:1, 0:64], T.st[:]), "ldtab", 16)
    done(S.dma_start(T.row[0:1, 64:128], T.ln[:]), "ldtab", 16)
    t_cd, t_tab = ("ldcd", 64), ("ldtab", 32)
    t_xa = done(Y.dma_start(T.xw[:, 0:XA], T.x[:, 0:XA]), "ldxa", 16)
    Y.wait_ge(T.sem.go, 1)
    t_xb = done(Y.dma_start(T.xw[:, XA:4 * XC], T.x[:, XA:4 * XC]), "ldxb", 16)
    t_qw = done(Y.dma_start(T.qt[:], T.qw[:]), "ldqw", 16)

    def iota(out, pattern, base=0):
        return done(g.iota(out, pattern, base, 0, allow_small_or_imprecise_dtypes=True), "gi")

    iota(T.lrow[:, 0:32], [[0, 2], [4, 16]])
    i_row = iota(T.lrow[:, 32:64], [[0, 2], [-4 * H, 4], [1, 4]], 12 * H - 8)
    i_pc = iota(T.pc[:], [[64, 2], [1, 4]])
    i_u16 = iota(T.u16[:], [[4, 16]])
    lane4, turn = T.lcol[:, 0:1], T.lcol[:, 32:33]

    t_0 = v(V.memset(T.cdl[HALF[1], :], 0))
    t_d = v(V.memset(T.D[:], -1.0))
    vneed(i_row)
    t = v(V.transpose(T.lcol[:], T.lrow[:]))
    vneed(t, i_pc)
    t_po = v(V.tensor_scalar(T.po[:], T.pc[:], lane4, None, ADD))
    vneed(i_u16)
    v(V.tensor_scalar(T.tri[:], T.u16[:], lane4, None, AluOpType.is_le))

    sneed(t_d)
    sc(S.activation(T.lim[:], T.D[:, W0:W0 + CAP], Identity, bias=-float(XC + 1), scale=0.0))
    sc(S.activation(T.neg[:], T.D[:, W0:W0 + 64], Identity, bias=LOW, scale=0.0))
    t_fill = sc(S.activation(T.mask[:], T.D[:, W0:W0 + 4 * WIN], Copy, scale=0.0))

    need("g", g, t_0, t_cd)
    g.remote_dma(T.lst[:, 0:1], T.cdl[:, part[0]:part[0] + 1], T.sem.lstA, T.sem.snt, addr[0][1], addr[0][0], bits(both))
    g.remote_dma_fused([RemoteDMATransfer(dst_ids=[dsts[s]], dma_engine_mask=bits(both[h * s - h:h * s]),
                                          remote_sem=T.sem.lstB, srcs=[T.cdl[:, part[s]:part[s] + 1]],
                                          dsts=[T.lst[:, s:s + 1]]) for s in (1, 2)], local_sem=T.sem.snt)
    nsent = [2 * ne]
    g.sem_inc(T.sem.go, 1)
    need("g", g, t_tab)
    i_bc = done(g.partition_broadcast(T.bc[:], T.row[0:1, :], 128), "gi")
    i_u4 = iota(T.u4[:], [[0, KO], [9 * H, 2], [5 * H, 2]], 8 - 16 * H)

    vneed(t_cd)
    v(V.tensor_copy(T.lo[HALF[1], 0:1], T.cdl[HALF[0], rank:rank + 1]))
    vneed(i_bc, t_po)
    t_t = v(V.tensor_copy(T.tab[:], T.bc[:].indirect(T.po[:])))
    stw, lnw = T.tab[:, 0:64], T.tab[:, 64:128]

    def win(buf, n, base=0):
        return buf[:, base:base + WIN * (n - 1) + CAP + 1]

    tk = {}
    grp = {"A": 0, "B": 1}
    start = {"A": NA, "B": NB}

    def col(buf, k):
        return buf[:, 2 * grp[k]:2 * grp[k] + 1]

    def doc(buf, k):
        return buf[:, 16 * grp[k]:16 * grp[k] + 16]

    def tok(buf, k):
        return buf[:, CAP * grp[k]:CAP * grp[k] + CAP]

    def table_ends(k):
        vneed(t_t)
        return v(V.tensor_tensor(T.end[:], stw, lnw, ADD))

    def table_hold(k):
        vneed(i_u4)
        return v(V.tensor_scalar(T.A[:], T.u4[:], turn, float(H), ADD, MIN))

    def listed(k):
        u, s = "AB"[k // 2], step_of[k]
        vneed(("lst" + u, ne))
        t = v(V.tensor_copy(T.lo[HALF[k % 2], 2 * grp[u]:2 * grp[u] + 1], T.lst[HALF[0], s:s + 1]))
        tk["l", u] = t
        if k != 2:
            sneed(t, t_t)
            tk["n", u] = sc(S.activation(T.D[:, start[u]:start[u] + 16], stw.indirect(col(T.lo, u)), Identity,
                                         bias=-1.0, scale=-1.0))
        return t

    def lengths(k):
        vneed(tk["l", k])
        return v(V.tensor_tensor(doc(T.MG, k), lnw.indirect(col(T.lo, k)), T.tri[:], MUL))

    def ends(k):
        vneed(tk["g", k], t_fill)
        return v(V.tensor_tensor_scan(doc(T.C, k), T.lim[:, 0:16], doc(T.MG, k), float(2 * WIN * grp[k]), MAX, ADD))

    def jumps(k):
        vneed(tk["n", k], tk["x", 0])
        return v(V.tensor_tensor(doc(T.J, k), T.end[:].indirect(col(T.lo, k)), T.D[:, start[k] + 1:start[k] + 17], ADD))

    def end_offsets(k):
        vneed(tk["c", k])
        t = v(V.tensor_copy(col(T.cL, k), T.C[:, 16 * grp[k] + 15:16 * grp[k] + 16]))
        need("g", g, t)
        g.remote_dma(col(T.cL, k), col(T.cL, k), T.sem["hends" + k], T.sem.snt, helper[1], helper[0], bits(near))
        nsent[0] += len(near)
        return t

    def spread(k):
        vneed(tk["e", k], tk["j", k])
        window = win(T.D, 1) if k == "A" else win(T.D, 3, W0)
        return v(V.tensor_copy(window.indirect(col(T.cL, k)), doc(T.J, k)))

    def run(k):
        vneed(tk["s", k])
        w = 0 if k == "A" else W0 + 2 * WIN
        return v(V.tensor_tensor_scan(tok(T.SS, k), T.D[:, w:w + CAP], T.lim[:], T.D[:, start[k]:start[k] + 1], ADD, MAX))

    def hold(k):
        vneed(tk["r", k], tk["y", 0])
        return v(V.tensor_tensor_scan(tok(T.XX, k), T.A[:], tok(T.SS, k), 0.0, ADD, MAX))

    def codes(s):
        k = list_of[s]
        return T.lc[:, CAP * s:CAP * s + CAP], T.qc[:, CAP * k:CAP * k + CAP]

    def plane(s):
        k = list_of[s]
        return T.lp[:, CAP * s:CAP * s + CAP], T.qs[:, CAP * k:CAP * k + CAP]

    def piece(k, a, b):
        return (T.tile[:, 4 * CAP * k + 16 * a:4 * CAP * k + 16 * b], T.xw[:].indirect(T.O[:, KO * k + a:KO * k + b]))

    def offsets(k):
        u, src = k // 2, HALF[k % 2]
        vneed(tk["h", "AB"[u]])
        for out in HALF:
            t = v(V.tensor_scalar(T.O[out, KO * k:KO * k + KO], T.XX[src, CAP * u + 3:CAP * u + CAP:4], -4.0,
                                  T.lcol[src, 32:33], MUL, ADD))
        sneed(t, t_xa, t_xb)
        o, i = piece(k, sum(CUT[k]), KO)
        tk["z", k] = sc(S.activation(o, i, Copy))
        return t

    taken = [0] * 4

    def gather(k):
        vneed(tk["o", k], t_xa, t_xb)
        a = sum(CUT[k][:taken[k]])
        o, i = piece(k, a, a + CUT[k][taken[k]])
        taken[k] += 1
        return v(V.tensor_copy(o, i))

    def quant(k):
        vneed(tk["v", k], tk["z", k])
        t = v(V.quantize_mx(T.qc[:, CAP * k:CAP * k + CAP], T.qs[:, CAP * k:CAP * k + CAP],
                            T.tile[:, 4 * CAP * k:4 * CAP * (k + 1)]))
        if k != OWN:
            s = step_of[k]
            need("g", g, t)
            o, i = [a.bitcast(dt.uint8) for a in codes(s)]
            g.remote_dma(o, i, T.sem["arr%d" % s], T.sem.snt, addr[s][1], addr[s][0], bits(both))
            o, i = plane(s)
            if s:
                g.remote_dma(o, i, T.sem["arr%d" % s], T.sem.snt, addr[s][1], addr[s][0], bits(both))
            else:
                g.remote_dma(o, i, T.sem.hplane, T.sem.snt, helper[1], helper[0], bits(near))
            nsent[0] += ne + (ne if s else len(near))
        return t

    def queries(k):
        vneed(t_qw)
        return v(V.quantize_mx(T.qwc[:], T.qws[:], T.qt[:]))

    def marks(k):
        vneed(("sel", 2 * ne))
        return v(V.tensor_copy(win(T.mask, 4).indirect(T.seL[:, 0:4]), T.neg[:]))

    step = {"x": table_ends, "y": table_hold, "l": listed, "g": lengths, "c": ends, "j": jumps, "e": end_offsets,
            "s": spread, "r": run, "h": hold, "o": offsets, "v": gather, "q": quant,
            "w": queries, "m": marks}
    for name in ORDER:
        k = name[1] if name[1] in grp else int(name[1])
        tk[name[0], k] = step[name[0]](k)

    def product(k):
        if k == OWN:
            need("p", P, tk["w", 0], tk["q", k])
            rc, rp = T.qc[:, CAP * k:CAP * k + CAP], T.qs[:, CAP * k:CAP * k + CAP]
        else:
            s = step_of[k]
            need("p", P, tk["w", 0], ("arr%d" % s, 2 * ne))
            rc, rp = codes(s)[0], plane(s)[0]
        t = done(P.matmul_mx(T.ps[:, 512 * k:512 * k + CAP], T.qwc[:], T.qws[:], rc, rp, True, True), "pe")
        vneed(t, tk["m", 0])
        z = W0 + WIN * k + 1
        return v(V.tensor_tensor_scan(T.D[:, z:z + CAP], T.mask[:, WIN * k:WIN * k + CAP],
                                      T.ps[:, 512 * k:512 * k + CAP], LOW, ADD, MAX))

    z = {k: product(k) for k in (OWN, 2, 0, 3)}
    for a in (0, 2):
        vneed(z[a], z[a + 1])
        q = (part[a] // 2) * 2
        t = v(V.tensor_copy(T.yo[:, CD * q:CD * q + 2 * CD], win(T.D, a + 2, W0).indirect(T.seL[:, q:q + 2])))
        need("y", Y, t)
        done(Y.dma_start(T.y[:, CD * q:CD * q + 2 * CD], T.yo[:, CD * q:CD * q + 2 * CD]), "yst", 16)
    need("y", Y, ("yst", 32))
    need("g", g, ("snt", nsent[0]))
